import numpy as np, ml_dtypes
CORES = [3,11,19,27,35,43]
N = 6
import mx_ref
BF = ml_dtypes.bfloat16
def entries(a):
    return np.ascontiguousarray(a.T).reshape(-1)
def table(e):
    return np.ascontiguousarray(np.reshape(e, (-1, 16)).T).astype(np.int32)
def f(rng, *shape):
    return mx_ref.flush((rng.standard_normal(shape, dtype=np.float32) * np.exp2(rng.integers(-2, 3, shape[:-1] + (1,)))).astype(BF))
def wide(rng, *shape, cols=0):
    v = rng.standard_normal(shape, dtype=np.float32) * np.exp2(rng.integers(-12, 13, shape)).astype(np.float32)
    if cols: v *= np.repeat(np.exp2(rng.integers(-cols, cols + 1, shape[:-2] + (1, shape[-1] // 4))) * (rng.random(shape[:-2] + (1, shape[-1] // 4)) > 0.0625), 4, axis=-1).astype(np.float32)
    return mx_ref.flush(v.astype(BF))
T, ND, CD, LM, CAPP = 768, 64, 16, 64, 160
def lens(rng, n, total):
    a = 1 + np.minimum(LM - 1, rng.multinomial(total - n, rng.dirichlet(np.ones(n))))
    for i in rng.permutation(n): a[i] += min(LM - a[i], total - a.sum())
    return a
def places(rng, l):
    o = rng.permutation(ND); g = rng.multinomial(T - l.sum(), rng.dirichlet(np.ones(ND + 1)))
    s = np.zeros(ND, int); s[o] = np.cumsum(g[:ND]) + np.cumsum(l[o]) - l[o]
    return s
def pick(rng, l):
    p = rng.permutation(ND); a, b = p[:CD].copy(), p[CD:].copy()
    while l[a].sum() > CAPP:
        i = np.argmax(l[a]); j = rng.choice(np.flatnonzero(l[b] < l[a[i]]))
        a[i], b[j] = b[j], a[i]
    return rng.permutation(a)
def lists(rng, kind="any"):
    s, n, c = [], [], np.zeros((N, N * CD), int)
    K, J = (T - ND) // (LM - 1), (CAPP - CD) // (LM - 1)
    TT = min(T, ND // CD * CAPP)
    for q in range(N):
        d = rng.permutation(ND); l = np.ones(ND, int)
        if kind == "long": l[d[:K]] = LM
        elif kind == "full": l[d] = np.concatenate([lens(rng, CD, CAPP), lens(rng, CD, CAPP), lens(rng, ND - 2 * CD, T - 2 * CAPP)])
        elif kind == "any": l[d] = lens(rng, ND, int(rng.integers(TT - TT // 4, TT + 1)))
        s.append(table(places(rng, l))); n.append(table(l))
        for r in range(N):
            if kind == "long": e = rng.permutation(np.concatenate([rng.permutation(d[:K])[:J], rng.permutation(d[K:])[:CD - J]]))
            elif kind == "full": k = CD * int(rng.integers(0, 2)); e = rng.permutation(d[k:k + CD])
            else: e = pick(rng, l)
            c[r, CD * q:CD * q + CD] = e
    return {"st": np.stack(s), "ln": np.stack(n), "cd": np.stack([table(c[r]) for r in range(N)])}
def setup_inputs(rng):
    return {"x": f(rng, N, 128, 4 * T), "qw": f(rng, N, 128, 512), **lists(rng)}
def setup_inputs_long(rng):
    return {**setup_inputs(rng), **lists(rng, "long")}
def setup_inputs_ones(rng):
    return {**setup_inputs(rng), **lists(rng, "ones")}
def setup_inputs_full(rng):
    return {**setup_inputs(rng), **lists(rng, "full")}
def setup_inputs_below(rng):
    d = setup_inputs(rng); p = rng.permutation(N)
    s, u = rng.integers(-20, 27, N), rng.integers(-20, 28, N)
    s[p[0]] = 26; u[rng.choice(p[:-1])] = 27; s[p[-1]] = 0; u[p[-1]] = 0
    d["x"] = mx_ref.flush((-np.exp2(rng.uniform(-3, 3, (N, 128, 4 * T)) + s[:, None, None])).astype(BF))
    d["qw"] = mx_ref.flush(np.exp2(rng.uniform(-2, 2, (N, 128, 512)) + u[:, None, None]).astype(BF))
    return d
def setup_inputs_spread(rng):
    d = setup_inputs(rng); d["x"] = wide(rng, N, 128, 4 * T, cols=8); return d
def check_inputs(d):
    b = []
    L = [entries(d["ln"][r]).astype(np.int64) for r in range(N)]
    for r in range(N):
        s, l = entries(d["st"][r]).astype(np.int64), L[r]
        if l.min() < 1 or l.max() > LM: b.append("ln")
        o = np.argsort(s, kind="stable")
        if s.min() < 0 or (s + l).max() > T or (s[o][:-1] + l[o][:-1] > s[o][1:]).any(): b.append("st")
        c = entries(d["cd"][r])
        if c.min() < 0 or c.max() >= ND: b.append("cd"); continue
        for q in range(N):
            e = c[CD * q:CD * q + CD]
            if len(set(e.tolist())) != CD or L[q][e].sum() > CAPP: b.append("cd")
    return sorted(set(b))
def reference(x, qw, st, ln, cd):
    X = [mx_ref.quantize(x[q]) for q in range(N)]
    y = np.zeros((N, 128, N * CD), np.float32)
    for r in range(N):
        W = mx_ref.quantize(qw[r]); c = entries(cd[r])
        for q in range(N):
            z = mx_ref.matmul(W, X[q]); s, l = entries(st[q]), entries(ln[q])
            for i in range(CD * q, CD * q + CD):
                y[r][:, i] = z[:, s[c[i]]:s[c[i]] + l[c[i]]].max(axis=1)
    return {"y": y}

@@ -1,0 +1,322 @@
+import numpy as np
+from concourse.bass import DstId, RemoteDMATransfer
+from concourse.mybir import dt, AluOpType, ActivationFunctionType
+
+N, CD, ND, TOK, CAP = 6, 16, 64, 768, 160
+S = N - 1
+VW = CAP + 8
+XW = 4 * (TOK + CAP)
+OW = 4 * CAP // 16
+RAMP = 4096
+BIG = 1.0e29
+LISTS = [(0, 1), (1, S), (S, N)]
+CUT = [24, 26, 32, 28, 32, 40]
+OWN_AT = 3
+EARLY = "l2 g2 e2 n2 d2".split()
+ORDER = ("i g0 l0 e0 g1 n0 d0 e1 l1 s0 d1 n1 p0 s1 s3 h0 s2 p1 c0 p2 h1 v0 c1 h2 p3 q0 c2 v1 s4 h3 q1 p4 c3 v2 h4 s5 "
+         "q2 c4 v3 p5 q3 h5 v4 c5 q4 m q5").split()
+
+SCRATCH = {
+    "cdi": ("sbuf", [128, N], "int32"),
+    "cdu": ("sbuf", [128, N], "uint16"),
+    "cdl": ("sbuf", [128, N * S + 2], "uint16"),
+    "cdx": ("sbuf", [128, 4], "uint16"),
+    "cdown": ("sbuf", [128, 2], "uint16"),
+    "raw": ("sbuf", [128, 2 * ND], "int32"),
+    "bc": ("sbuf", [128, 2 * ND], "int32"),
+    "tabs": ("sbuf", [128, ND], "float32"),
+    "tabl": ("sbuf", [128, ND], "float32"),
+    "tabm": ("sbuf", [128, ND], "float32"),
+    "tabe": ("sbuf", [128, ND], "float32"),
+    "ip": ("sbuf", [128, 1], "int32"),
+    "ii": ("sbuf", [128, 4], "int32"),
+    "pf": ("sbuf", [128, 4], "float32"),
+    "it16": ("sbuf", [128, N * CD], "float32"),
+    "it4": ("sbuf", [128, CAP], "float32"),
+    "itr": ("sbuf", [128, CAP], "float32"),
+    "tri": ("sbuf", [128, N * CD], "float32"),
+    "rst": ("sbuf", [128, N * CD], "float32"),
+    "hold": ("sbuf", [128, CAP], "float32"),
+    "inc": ("sbuf", [128, CAP], "float32"),
+    "neg": ("sbuf", [128, CD], "float32"),
+    "lm": ("sbuf", [128, N * CD], "float32"),
+    "cs": ("sbuf", [128, N * CD + 8], "uint16"),
+    "sg": ("sbuf", [128, N * CD], "float32"),
+    "eg": ("sbuf", [128, N * CD + 8], "float32"),
+    "dg": ("sbuf", [128, N * CD + 8], "float32"),
+    "v": ("sbuf", [128, N * VW], "float32"),
+    "f": ("sbuf", [128, N * CAP], "float32"),
+    "a": ("sbuf", [128, N * CAP], "float32"),
+    "off": ("sbuf", [128, N * OW], "uint16"),
+    "xs": ("sbuf", [128, XW], "bfloat16"),
+    "h": ("sbuf", [128, N * 4 * CAP], "bfloat16"),
+    "qwb": ("sbuf", [128, 512], "bfloat16"),
+    "wq": ("sbuf", [128, 128], "float8_e4m3fn_x4"),
+    "wp": ("sbuf", [128, 128], "uint8"),
+    "q": ("sbuf", [128, N * CAP], "float8_e4m3fn_x4"),
+    "p": ("sbuf", [128, N * CAP], "uint8"),
+    "rc": ("sbuf", [128, N * CAP], "float8_e4m3fn_x4"),
+    "rp": ("sbuf", [128, N * CAP], "uint8"),
+    "cl": ("sbuf", [128, 2 * N], "uint16"),
+    "m": ("sbuf", [128, N * VW], "float32"),
+    "z": ("sbuf", [128, N * VW], "float32"),
+    "ys": ("sbuf", [128, N * CD], "float32"),
+    "ps": ("psum", [128, 512 * N], "float32"),
+}
+SEMAPHORES = ["dc", "dr", "dx", "dq", "dy", "gi", "vv", "aa", "tt", "ls", "rq", "cc"] \
+    + ["co%d" % i for i in range(N)] + ["pl%d" % i for i in range(N)]
+
+
+def order_of(r, T, topo):
+    chip = [topo.chip(c) for c in T.cores]
+    mate = [[j for j in range(N) if topo.mates(chip[i], chip[j])][0] for i in range(N)]
+    plane = sorted([j for j in range(N) if topo.same_plane(chip[r], chip[j])], key=lambda j: (j - r) % N)
+    far = [mate[j] for j in plane]
+    o = []
+    for k in range(len(plane)):
+        o += [far[k], plane[len(plane) - 1 - k]]
+    return o + [mate[r]]
+
+
+def rank_program(g, core, T, topo):
+    rank = T.rank_of(core)
+    if rank is None:
+        return
+    op, act = AluOpType, ActivationFunctionType
+    V, A, E, Y = g.vector, g.scalar, g.tensor, g.sync
+    sem = T.sem
+    orders = [order_of(r, T, topo) for r in range(N)]
+    order = orders[rank]
+    pos_at = [orders[d].index(rank) if d != rank else None for d in range(N)]
+    src = [[r for r in range(N) if r != rank and orders[r][s] == rank][0] for s in range(S)]
+
+    def bits(es):
+        return sum(1 << e for e in es)
+    eng = [topo.engines(core, T.cores[d]) for d in order]
+    ids = []
+    for d in order:
+        a = topo.addr(T.cores[d])
+        ids.append(DstId(rid=a[0], pnc=a[1]))
+    ne = len(eng[0])
+    share = [ne // 4] * 4 + [ne]
+
+    vn, vw, an, tn, gn, ln_ = [0], [0], [0], [0], [0], [0]
+
+    def v(ins):
+        ins.then_inc(sem.vv, 1)
+        vn[0] += 1
+        return vn[0]
+
+    def vneed(n):
+        if n > vw[0]:
+            V.wait_ge(sem.vv, n)
+            vw[0] = n
+
+    def a_(ins):
+        ins.then_inc(sem.aa, 1)
+        an[0] += 1
+        return an[0]
+
+    def gi(ins):
+        ins.then_inc(sem.gi, 1)
+        gn[0] += 1
+        return gn[0]
+
+    for k in range(8):
+        (Y if k % 2 == 0 else A).dma_start(T.cdi[16 * k:16 * k + 16, 0:N], T.cd[:, :]).then_inc(sem.dc, 16)
+    Y.dma_start(T.raw[0:1, 0:ND], T.st[:, :]).then_inc(sem.dr, 16)
+    A.dma_start(T.raw[0:1, ND:2 * ND], T.ln[:, :]).then_inc(sem.dr, 16)
+    Y.dma_start(T.xs[:, 0:4 * TOK], T.x[:, :]).then_inc(sem.dx, 16)
+    A.dma_start(T.qwb[:, :], T.qw[:, :]).then_inc(sem.dq, 16)
+
+    gi(g.iota(T.ip[:, 0:1], [[1, 1]], 0, 1))
+    gi(g.iota(T.it16[:, :], [[0, N], [1, CD]], 0, 0, allow_small_or_imprecise_dtypes=True))
+    g_it = gi(g.iota(T.it4[:, :], [[0, CAP // 4], [1, 4]], 0, 0, allow_small_or_imprecise_dtypes=True))
+
+    v(V.memset(T.neg[:, :], -BIG))
+    v(V.memset(T.dg[:, :], 0.0))
+    V.wait_ge(sem.gi, g_it)
+    v(V.tensor_scalar(T.ii[:, 0:1], T.ip[:, 0:1], 15, None, op.bitwise_and))
+    v(V.tensor_scalar(T.ii[:, 1:2], T.ip[:, 0:1], 3, None, op.bitwise_and))
+    n = v(V.tensor_scalar(T.ii[:, 2:3], T.ip[:, 0:1], 15, 2, op.bitwise_and, op.logical_shift_right))
+    n2 = v(V.tensor_scalar(T.itr[:, :], T.it4[:, :], 1.0, 4.0 * RAMP, op.min, op.mult))
+    vneed(n)
+    n = v(V.tensor_copy(T.pf[:, 0:3], T.ii[:, 0:3]))
+    v(V.tensor_scalar(T.rst[:, :], T.it16[:, :], 1.0, None, op.min))
+    vneed(n2)
+    n2 = v(V.tensor_scalar(T.inc[:, :], T.itr[:, :], 4.0 - 3 * RAMP, None, op.add))
+    vneed(n)
+    v(V.tensor_scalar(T.tri[:, :], T.it16[:, :], T.pf[:, 0:1], None, op.is_le))
+    v(V.tensor_scalar(T.pf[:, 3:4], T.pf[:, 2:3], float(RAMP), T.pf[:, 1:2], op.mult, op.subtract))
+    v(V.tensor_scalar(T.hold[:, :], T.it4[:, :], T.pf[:, 2:3], 1.0e9, op.is_le, op.mult))
+    vneed(n2)
+    v(V.memset(T.inc[:, 0:1], 0.0))
+
+    V.wait_ge(sem.dc, 128)
+    v_cdu = v(V.tensor_copy(T.cdu[:, :], T.cdi[:, :]))
+    g.wait_ge(sem.vv, v_cdu)
+    g.remote_dma_fused([RemoteDMATransfer(
+        dst_ids=ids, dma_engine_mask=bits(eng[0]), remote_sem=sem.rq, srcs=[T.cdu[:, :]],
+        dsts=[T.cdl[:, N * pos_at[d] + d % 2:N * pos_at[d] + d % 2 + N] for d in order])], local_sem=sem.ls)
+    ln_[0] += ne
+    rq_total = sum(len(topo.engines(T.cores[d], core)) for d in order)
+
+    g.wait_ge(sem.dr, 32)
+    g_bc = gi(g.partition_broadcast(T.bc[:, :], T.raw[0:1, :], 128))
+
+    v(V.tensor_copy(T.cdown[:, 0:1], T.cdi[:, rank:rank + 1]))
+    v_zero = v(V.memset(T.v[:, :], 0.0))
+    v(V.memset(T.xs[:, 4 * TOK:XW], 0.0))
+    v(V.memset(T.m[:, :], BIG))
+    A.wait_ge(sem.vv, v_zero)
+    a_z = a_(A.activation(T.z[:, :], T.v[:, :], act.Copy))
+    V.wait_ge(sem.gi, g_bc)
+    for u in range(ND // 16):
+        v(V.tensor_copy(T.tabl[:, 16 * u:16 * u + 16], T.bc[:, ND + u:2 * ND:ND // 16]))
+        n = v(V.tensor_scalar(T.tabs[:, 16 * u:16 * u + 16], T.bc[:, u:ND:ND // 16], 4.0, None, op.mult))
+    vneed(n)
+    n = v(V.tensor_scalar(T.tabm[:, :], T.tabl[:, :], 4.0, None, op.mult))
+    V.wait_ge(sem.dq, 16)
+    v(V.quantize_mx(T.wq[:, :], T.wp[:, :], T.qwb[:, :]))
+    vneed(n)
+    vneed(v(V.tensor_tensor(T.tabe[:, :], T.tabs[:, :], T.tabm[:, :], op.add)))
+
+    def end_of(s):
+        return T.cs[:, CD * (s + 1):CD * (s + 1) + 1]
+
+    def places_of(d):
+        return end_of(S) if d == rank else T.cl[:, 2 * d:2 * d + 1]
+
+    first = rank + rank % 2
+    numbers = [T.cdl[:, first:first + 1], T.cdx[:, 0:S - 1], T.cdown[:, 0:1]]
+
+    def part(s, lo, hi):
+        return (T.h[:, 4 * CAP * s + 16 * lo:4 * CAP * s + 16 * hi],
+                T.xs[:, :].indirect(T.off[:, OW * s + lo:OW * s + hi]))
+
+    at, a_of = {}, {}
+
+    def work(word):
+        k = word[0]
+        s = int(word[1:] or 0)
+        c, w = slice(CAP * s, CAP * (s + 1)), slice(OW * s, OW * (s + 1))
+        if k == "i":
+            b = first + N
+            x = v(V.tensor_copy(T.cdx[:, 0:S - 1], T.cdl[:, b:b + N * (S - 2) + 1:N]))
+        elif k in "lgend":
+            lo, hi = CD * LISTS[s][0], CD * LISTS[s][1]
+            if k in "lge" and s == 1:
+                vneed(at["i"])
+            if k == "l":
+                x = v(V.tensor_tensor(T.lm[:, lo:hi], T.tabl[:, :].indirect(numbers[s]), T.tri[:, lo:hi], op.mult))
+            elif k == "g":
+                x = v(V.tensor_copy(T.sg[:, lo:hi], T.tabs[:, :].indirect(numbers[s])))
+            elif k == "e":
+                x = v(V.tensor_copy(T.eg[:, lo + 1:hi + 1], T.tabe[:, :].indirect(numbers[s])))
+            elif k == "n":
+                vneed(at["l%d" % s])
+                x = v(V.tensor_tensor_scan(T.cs[:, lo + 1:hi + 1], T.rst[:, lo:hi], T.lm[:, lo:hi], 0.0,
+                                           op.mult, op.add))
+            else:
+                vneed(max(at["g%d" % s], at["e%d" % s]))
+                x = v(V.tensor_tensor(T.dg[:, lo + 1:hi], T.sg[:, lo + 1:hi], T.eg[:, lo + 1:hi], op.subtract))
+        elif k == "s":
+            b = 0 if s == 0 else 2 if s == S else 1
+            vneed(max(at["n%d" % b], at["d%d" % b]))
+            x = v(V.tensor_copy(T.v[:, VW * s:VW * (s + 1)].indirect(end_of(s)), T.dg[:, CD * s + 1:CD * (s + 1) + 1]))
+        elif k == "p":
+            vneed(at["s%d" % s])
+            x = v(V.tensor_tensor_scan(T.f[:, c], T.inc[:, :], T.v[:, VW * s:VW * s + CAP],
+                                       T.sg[:, CD * s:CD * s + 1], op.add, op.add))
+        elif k == "h":
+            vneed(at["p%d" % s])
+            x = v(V.tensor_tensor_scan(T.a[:, c], T.hold[:, :], T.f[:, c], 0.0, op.max, op.min))
+        elif k == "c":
+            vneed(at["h%d" % s])
+            x = v(V.tensor_scalar(T.off[:, w], T.a[:, CAP * s + 3:CAP * (s + 1):4], T.pf[:, 3:4], None, op.subtract))
+            A.wait_ge(sem.vv, x)
+            o, i = part(s, 0, CUT[s])
+            a_of[s] = a_(A.activation(o, i, act.Copy))
+        elif k == "v":
+            vneed(at["c%d" % s])
+            o, i = part(s, CUT[s], OW)
+            x = v(V.tensor_copy(o, i))
+        elif k == "q":
+            V.wait_ge(sem.aa, a_of[s])
+            vneed(at.get("v%d" % s, 0))
+            x = v(V.quantize_mx(T.q[:, c], T.p[:, c], T.h[:, 4 * CAP * s:4 * CAP * (s + 1)]))
+        else:
+            V.wait_ge(sem.cc, sum(share))
+            for d in range(N):
+                x = v(V.tensor_copy(T.m[:, VW * d:VW * (d + 1)].indirect(places_of(d)), T.neg[:, :]))
+        at[word] = x
+
+    for word in EARLY:
+        work(word)
+    A.wait_ge(sem.dx, 16)
+    V.wait_ge(sem.dx, 16)
+    V.wait_ge(sem.aa, a_z)
+    V.wait_ge(sem.rq, rq_total)
+    for word in ORDER:
+        work(word)
+    vneed(at["m"])
+
+    def single(s, sm, o, i):
+        a = topo.addr(T.cores[order[s]])
+        g.remote_dma(o, i, remote_sem=sm, local_sem=sem.ls, pid=a[1], routing_id=a[0],
+                     dma_engine_mask=topo.mask(core, T.cores[order[s]]))
+        ln_[0] += len(eng[s])
+
+    my_end = T.cl[:, 2 * rank:2 * rank + 1]
+    g.wait_ge(sem.vv, max(at["n0"], at["n1"]))
+    ts = []
+    for s in range(4):
+        es = eng[s][share[s] * s:share[s] * (s + 1)]
+        ts.append(RemoteDMATransfer(dst_ids=[ids[s]], dma_engine_mask=bits(es), remote_sem=sem.cc,
+                                    srcs=[end_of(s)], dsts=[my_end]))
+        ln_[0] += len(es)
+    g.remote_dma_fused(ts, local_sem=sem.ls)
+    single(4, sem.cc, my_end, end_of(4))
+
+    land = slice(CAP * rank, CAP * (rank + 1))
+    for s in range(S):
+        mine = slice(CAP * s, CAP * (s + 1))
+        g.wait_ge(sem.vv, at["q%d" % s])
+        single(s, sem["co%d" % rank], T.rc[:, land].bitcast(dt.uint8), T.q[:, mine].bitcast(dt.uint8))
+        single(s, sem["pl%d" % rank], T.rp[:, land], T.p[:, mine])
+
+    t_of = {}
+
+    def product(b, cq, cp, k):
+        E.matmul_mx(T.ps[:, 512 * b:512 * b + CAP], T.wq[:, :], T.wp[:, :], cq[:, k:k + CAP], cp[:, k:k + CAP],
+                    True, True).then_inc(sem.tt, 1)
+        tn[0] += 1
+        t_of[b] = tn[0]
+    turn = src[:OWN_AT] + [rank] + src[OWN_AT:]
+    for d in turn:
+        if d == rank:
+            E.wait_ge(sem.vv, at["q%d" % S])
+            product(rank, T.q, T.p, CAP * S)
+        else:
+            if not t_of:
+                E.wait_ge(sem.vv, at["q0"])
+            E.wait_ge(sem["co%d" % d], len(topo.engines(T.cores[d], core)))
+            E.wait_ge(sem["pl%d" % d], len(topo.engines(T.cores[d], core)))
+            product(d, T.rc, T.rp, CAP * d)
+
+    for d in turn:
+        V.wait_ge(sem.tt, t_of[d])
+        n = v(V.tensor_tensor_scan(T.z[:, VW * d + 1:VW * d + CAP + 1], T.m[:, VW * d:VW * d + CAP],
+                                   T.ps[:, 512 * d:512 * d + CAP], -BIG, op.min, op.max))
+        o, i = T.ys[:, CD * d:CD * (d + 1)], T.z[:, VW * d:VW * (d + 1)].indirect(places_of(d))
+        if d != turn[-1]:
+            A.wait_ge(sem.vv, n)
+            a_(A.activation(o, i, act.Copy))
+        else:
+            vneed(n)
+            n = v(V.tensor_copy(o, i))
+    Y.wait_ge(sem.aa, an[0])
+    Y.wait_ge(sem.vv, n)
+    Y.dma_start(T.y[:, :], T.ys[:, :]).then_inc(sem.dy, 16)
+    Y.wait_ge(sem.dy, 16)
+    g.wait_ge(sem.ls, ln_[0])

@@ -7,46 +7,52 @@ S = N - 1
 VW = CAP + 8
 XW = 4 * (TOK + CAP)
 OW = 4 * CAP // 16
-RAMP = 4096
+MW = 2 * CAP + 16
+LW = 2 * N
+XA = 4 * TOK
+RAMP = 1024
 BIG = 1.0e29
-LISTS = [(0, 1), (1, S), (S, N)]
-CUT = [24, 26, 32, 28, 32, 40]
-OWN_AT = 3
-EARLY = "l2 g2 e2 n2 d2".split()
-ORDER = ("i g0 l0 e0 g1 n0 d0 e1 l1 s0 d1 n1 p0 s1 s3 h0 s2 p1 c0 p2 h1 v0 c1 h2 p3 q0 c2 v1 s4 h3 q1 p4 c3 v2 h4 s5 "
-         "q2 c4 v3 p5 q3 h5 v4 c5 q4 m q5").split()
+LISTS = [(0, 1), (1, 2), (2, S), (S, N)]
+CUT = [40, 24, 40, 24, 22, 40]
+ENDS = [[1, 2, 3, 4]]
+OWN_AT = 0
+VIA = [["e0", "c0", "p0"]]
+TURN = [1, 2, S, 0, 3, 4]
+OWN = 8
+EARLY = "M2 M1 l3 g3 e3 n3 d3 o s5 p5 h5 c5".split()
+ORDER = ("g0 e0 l0 g1 e1 l1 n0 n1 d0 i g2 e2 b5 s0 d1 l2 p0 s1 h0 d2 c0 a0 n2 p1 s2 s3 s4 h1 p2 c1 a1 p3 h2 p4 c2 a2 "
+         "q0 h3 v1 h4 c3 a3 q1 c4 a4 a5 v3 q2 v4 q3 u w q4 m").split()
 
 SCRATCH = {
     "cdi": ("sbuf", [128, N], "int32"),
     "cdu": ("sbuf", [128, N], "uint16"),
-    "cdl": ("sbuf", [128, N * S + 2], "uint16"),
+    "cdl": ("sbuf", [128, LW * S], "uint16"),
     "cdx": ("sbuf", [128, 4], "uint16"),
     "cdown": ("sbuf", [128, 2], "uint16"),
     "raw": ("sbuf", [128, 2 * ND], "int32"),
     "bc": ("sbuf", [128, 2 * ND], "int32"),
     "tabs": ("sbuf", [128, ND], "float32"),
     "tabl": ("sbuf", [128, ND], "float32"),
-    "tabm": ("sbuf", [128, ND], "float32"),
     "tabe": ("sbuf", [128, ND], "float32"),
-    "ip": ("sbuf", [128, 1], "int32"),
-    "ii": ("sbuf", [128, 4], "int32"),
+    "ip": ("sbuf", [128, 4], "int32"),
+    "ii": ("sbuf", [128, 8], "int32"),
+    "turn": ("sbuf", [128, 4], "uint16"),
     "pf": ("sbuf", [128, 4], "float32"),
-    "it16": ("sbuf", [128, N * CD], "float32"),
+    "it16": ("sbuf", [128, 4 * CD], "float32"),
     "it4": ("sbuf", [128, CAP], "float32"),
-    "itr": ("sbuf", [128, CAP], "float32"),
-    "tri": ("sbuf", [128, N * CD], "float32"),
-    "rst": ("sbuf", [128, N * CD], "float32"),
-    "hold": ("sbuf", [128, CAP], "float32"),
+    "tri": ("sbuf", [128, 4 * CD], "float32"),
+    "rst": ("sbuf", [128, 4 * CD], "float32"),
+    "hold": ("sbuf", [128, CAP], "bfloat16"),
     "inc": ("sbuf", [128, CAP], "float32"),
-    "neg": ("sbuf", [128, CD], "float32"),
+    "neg": ("sbuf", [128, 2 * CD], "bfloat16"),
     "lm": ("sbuf", [128, N * CD], "float32"),
     "cs": ("sbuf", [128, N * CD + 8], "uint16"),
     "sg": ("sbuf", [128, N * CD], "float32"),
     "eg": ("sbuf", [128, N * CD + 8], "float32"),
     "dg": ("sbuf", [128, N * CD + 8], "float32"),
     "v": ("sbuf", [128, N * VW], "float32"),
-    "f": ("sbuf", [128, N * CAP], "float32"),
-    "a": ("sbuf", [128, N * CAP], "float32"),
+    "f": ("sbuf", [128, N * CAP], "uint16"),
+    "a": ("sbuf", [128, N * CAP], "uint16"),
     "off": ("sbuf", [128, N * OW], "uint16"),
     "xs": ("sbuf", [128, XW], "bfloat16"),
     "h": ("sbuf", [128, N * 4 * CAP], "bfloat16"),
@@ -57,14 +63,16 @@ SCRATCH = {
     "p": ("sbuf", [128, N * CAP], "uint8"),
     "rc": ("sbuf", [128, N * CAP], "float8_e4m3fn_x4"),
     "rp": ("sbuf", [128, N * CAP], "uint8"),
-    "cl": ("sbuf", [128, 2 * N], "uint16"),
-    "m": ("sbuf", [128, N * VW], "float32"),
-    "z": ("sbuf", [128, N * VW], "float32"),
+    "hl": ("sbuf", [128, 2], "uint16"),
+    "cl": ("sbuf", [128, 8 * N], "uint16"),
+    "ce": ("sbuf", [128, N], "uint16"),
+    "m": ("sbuf", [128, 16 + MW * (N // 2)], "bfloat16"),
+    "z": ("sbuf", [128, N * CAP], "float32"),
     "ys": ("sbuf", [128, N * CD], "float32"),
     "ps": ("psum", [128, 512 * N], "float32"),
 }
-SEMAPHORES = ["dc", "dr", "dx", "dq", "dy", "gi", "vv", "aa", "tt", "ls", "rq", "cc"] \
-    + ["co%d" % i for i in range(N)] + ["pl%d" % i for i in range(N)]
+SEMAPHORES = ["dc", "dr", "dx", "dq", "dy", "gi", "vv", "aa", "tt", "ls", "ll", "cc", "he", "dl"] \
+    + [k + str(i) for k in ("rq", "co", "pl") for i in range(N)]
 
 
 def order_of(r, T, topo):
@@ -78,151 +86,219 @@ def order_of(r, T, topo):
     return o + [mate[r]]
 
 
+def helpers_of(r, T, topo):
+    c = T.cores[r]
+    return [h for h in topo.cores_of(c) if topo.die(h) != topo.die(c) and all(topo.may_write(h, d) for d in T.cores)]
+
+
+def bits(es):
+    return sum(1 << e for e in es)
+
+
+def dst_id(c, topo):
+    a = topo.addr(c)
+    return DstId(rid=a[0], pnc=a[1])
+
+
+def write(g, T, topo, to, es, sm, o, i):
+    a = topo.addr(to)
+    g.remote_dma(o, i, remote_sem=sm, local_sem=T.sem.ls, pid=a[1], routing_id=a[0], dma_engine_mask=bits(es))
+    return len(es)
+
+
+def spare(core, to, far, topo):
+    return [e for e in topo.engines(core, to) if e not in topo.engines(core, far)]
+
+
+def helper_program(g, core, r, k, T, topo):
+    order = order_of(r, T, topo)
+    land = slice(CAP * r, CAP * (r + 1))
+    n = 0
+    for word in VIA[k]:
+        s = int(word[1])
+        to = T.cores[order[s]]
+        es = topo.engines(core, to)
+        ne = len(spare(T.cores[r], core, to, topo))
+        mine = slice(CAP * s, CAP * (s + 1))
+        if word[0] == "e":
+            g.wait_ge(T.sem.he, ne // len(VIA))
+            n += write(g, T, topo, to, es, T.sem.cc, T.cl[:, 8 * r:8 * r + 1], T.hl[:, 0:1])
+        elif word[0] == "c":
+            g.wait_ge(T.sem["co%d" % s], ne)
+            n += write(g, T, topo, to, es, T.sem["co%d" % r], T.rc[:, land].bitcast(dt.uint8),
+                       T.q[:, mine].bitcast(dt.uint8))
+        else:
+            g.wait_ge(T.sem["pl%d" % s], ne)
+            n += write(g, T, topo, to, es, T.sem["pl%d" % r], T.rp[:, land], T.p[:, mine])
+    g.wait_ge(T.sem.ls, n)
+
+
 def rank_program(g, core, T, topo):
     rank = T.rank_of(core)
     if rank is None:
+        for r in range(N):
+            hs = helpers_of(r, T, topo)[:len(VIA)]
+            if core in hs:
+                helper_program(g, core, r, hs.index(core), T, topo)
         return
     op, act = AluOpType, ActivationFunctionType
     V, A, E, Y = g.vector, g.scalar, g.tensor, g.sync
     sem = T.sem
     orders = [order_of(r, T, topo) for r in range(N)]
     order = orders[rank]
-    pos_at = [orders[d].index(rank) if d != rank else None for d in range(N)]
     src = [[r for r in range(N) if r != rank and orders[r][s] == rank][0] for s in range(S)]
+    helpers = helpers_of(rank, T, topo)
+    far = topo.engines(core, T.cores[order[0]])
+    near = spare(core, helpers[0], T.cores[order[0]], topo)
+    ne = len(far)
+    ends_by = [int(words[0][1]) for words in VIA if words[0][0] == "e"]
 
-    def bits(es):
-        return sum(1 << e for e in es)
-    eng = [topo.engines(core, T.cores[d]) for d in order]
-    ids = []
-    for d in order:
-        a = topo.addr(T.cores[d])
-        ids.append(DstId(rid=a[0], pnc=a[1]))
-    ne = len(eng[0])
-    share = [ne // 4] * 4 + [ne]
-
-    vn, vw, an, tn, gn, ln_ = [0], [0], [0], [0], [0], [0]
+    vn, vw, an, aw, av, va, tn, gn, ln_ = [0], [0], [0], [0], [0], [0], [0], [0], [0]
 
     def v(ins):
         ins.then_inc(sem.vv, 1)
         vn[0] += 1
         return vn[0]
 
-    def vneed(n):
-        if n > vw[0]:
-            V.wait_ge(sem.vv, n)
-            vw[0] = n
-
     def a_(ins):
         ins.then_inc(sem.aa, 1)
         an[0] += 1
         return an[0]
+
+    def need(Q, sm, seen, n):
+        if n > seen[0]:
+            Q.wait_ge(sm, n)
+            seen[0] = n
+
+    def vneed(n):
+        need(V, sem.vv, vw, n)
 
     def gi(ins):
         ins.then_inc(sem.gi, 1)
         gn[0] += 1
         return gn[0]
 
+    A.dma_start(T.raw[0:1, ND:2 * ND], T.ln[:, :]).then_inc(sem.dr, 16)
+    Y.dma_start(T.raw[0:1, 0:ND], T.st[:, :]).then_inc(sem.dr, 16)
     for k in range(8):
         (Y if k % 2 == 0 else A).dma_start(T.cdi[16 * k:16 * k + 16, 0:N], T.cd[:, :]).then_inc(sem.dc, 16)
-    Y.dma_start(T.raw[0:1, 0:ND], T.st[:, :]).then_inc(sem.dr, 16)
-    A.dma_start(T.raw[0:1, ND:2 * ND], T.ln[:, :]).then_inc(sem.dr, 16)
-    Y.dma_start(T.xs[:, 0:4 * TOK], T.x[:, :]).then_inc(sem.dx, 16)
-    A.dma_start(T.qwb[:, :], T.qw[:, :]).then_inc(sem.dq, 16)
+    Y.dma_start(T.xs[:, 0:XA], T.x[:, 0:XA]).then_inc(sem.dx, 16)
 
-    gi(g.iota(T.ip[:, 0:1], [[1, 1]], 0, 1))
-    gi(g.iota(T.it16[:, :], [[0, N], [1, CD]], 0, 0, allow_small_or_imprecise_dtypes=True))
+    g_ip = gi(g.iota(T.ip[:, :], [[1, 4]], 0, 4))
+    gi(g.iota(T.it16[:, :], [[0, 4], [1, CD]], 0, 0, allow_small_or_imprecise_dtypes=True))
     g_it = gi(g.iota(T.it4[:, :], [[0, CAP // 4], [1, 4]], 0, 0, allow_small_or_imprecise_dtypes=True))
 
-    v(V.memset(T.neg[:, :], -BIG))
+    v_zero = v(V.memset(T.xs[:, 4 * TOK:XW], 0.0))
+    V.wait_ge(sem.gi, g_ip)
+    v(V.tensor_scalar(T.ii[:, 0:1], T.ip[:, 0:1], 2, 15, op.logical_shift_right, op.bitwise_and))
+    v(V.tensor_scalar(T.ii[:, 1:2], T.ip[:, 0:1], 2, 3, op.logical_shift_right, op.bitwise_and))
+    v(V.tensor_scalar(T.ii[:, 2:3], T.ip[:, 0:1], 4, 3, op.logical_shift_right, op.bitwise_and))
+    n = v(V.tensor_scalar(T.ii[:, 4:8], T.ip[:, :], ND - 1, None, op.bitwise_and))
     v(V.memset(T.dg[:, :], 0.0))
-    V.wait_ge(sem.gi, g_it)
-    v(V.tensor_scalar(T.ii[:, 0:1], T.ip[:, 0:1], 15, None, op.bitwise_and))
-    v(V.tensor_scalar(T.ii[:, 1:2], T.ip[:, 0:1], 3, None, op.bitwise_and))
-    n = v(V.tensor_scalar(T.ii[:, 2:3], T.ip[:, 0:1], 15, 2, op.bitwise_and, op.logical_shift_right))
-    n2 = v(V.tensor_scalar(T.itr[:, :], T.it4[:, :], 1.0, 4.0 * RAMP, op.min, op.mult))
+    v(V.memset(T.neg[:, :], -BIG))
     vneed(n)
     n = v(V.tensor_copy(T.pf[:, 0:3], T.ii[:, 0:3]))
+    v(V.tensor_copy(T.turn[:, :], T.ii[:, 4:8]))
+    V.wait_ge(sem.gi, g_ip + 1)
     v(V.tensor_scalar(T.rst[:, :], T.it16[:, :], 1.0, None, op.min))
-    vneed(n2)
-    n2 = v(V.tensor_scalar(T.inc[:, :], T.itr[:, :], 4.0 - 3 * RAMP, None, op.add))
-    vneed(n)
+    vneed(n + 1)
     v(V.tensor_scalar(T.tri[:, :], T.it16[:, :], T.pf[:, 0:1], None, op.is_le))
-    v(V.tensor_scalar(T.pf[:, 3:4], T.pf[:, 2:3], float(RAMP), T.pf[:, 1:2], op.mult, op.subtract))
-    v(V.tensor_scalar(T.hold[:, :], T.it4[:, :], T.pf[:, 2:3], 1.0e9, op.is_le, op.mult))
-    vneed(n2)
-    v(V.memset(T.inc[:, 0:1], 0.0))
+    v(V.tensor_scalar(T.pf[:, 3:4], T.pf[:, 2:3], 4.0 * RAMP, T.pf[:, 1:2], op.mult, op.subtract))
 
-    V.wait_ge(sem.dc, 128)
-    v_cdu = v(V.tensor_copy(T.cdu[:, :], T.cdi[:, :]))
-    g.wait_ge(sem.vv, v_cdu)
-    g.remote_dma_fused([RemoteDMATransfer(
-        dst_ids=ids, dma_engine_mask=bits(eng[0]), remote_sem=sem.rq, srcs=[T.cdu[:, :]],
-        dsts=[T.cdl[:, N * pos_at[d] + d % 2:N * pos_at[d] + d % 2 + N] for d in order])], local_sem=sem.ls)
-    ln_[0] += ne
-    rq_total = sum(len(topo.engines(T.cores[d], core)) for d in order)
+    need(A, sem.vv, av, v_zero)
+
+    def fill(o, n, c):
+        i = T.xs[:, 4 * TOK:4 * TOK + n]
+        return a_(A.activation(o, i, act.Identity, bias=c) if c else A.activation(o, i, act.Copy))
+    fill(T.v[:, 0:2 * VW], 2 * VW, 0.0)
+    fill(T.inc[:, 0:1], 1, 0.0)
+    fill(T.inc[:, 4:CAP:4], CAP // 4 - 1, 1.0 - 3 * RAMP)
+    for u in range(1, 4):
+        a_inc = fill(T.inc[:, u:CAP:4], CAP // 4, 1.0 + RAMP)
 
     g.wait_ge(sem.dr, 32)
     g_bc = gi(g.partition_broadcast(T.bc[:, :], T.raw[0:1, :], 128))
 
+    V.wait_ge(sem.dc, 128)
+    v_cdu = v(V.tensor_copy(T.cdu[:, :], T.cdi[:, :]))
+    g.wait_ge(sem.vv, v_cdu)
+    at_d = [LW * s + N - d for s, d in enumerate(src)]
+    nl = ne
+    for lo, hi, es in ((0, S, far),):
+        g.remote_dma_fused([RemoteDMATransfer(
+            dst_ids=[dst_id(T.cores[d], topo) for d in src[lo:hi]], dma_engine_mask=bits(es),
+            remote_sem=sem["rq%d" % rank], srcs=[T.cdu[:, :]], dsts=[T.cdl[:, b:b + N] for b in at_d[lo:hi]])],
+            local_sem=sem.ll)
+    Y.wait_ge(sem.ll, ne)
+    Y.dma_start(T.qwb[:, :], T.qw[:, :]).then_inc(sem.dq, 16)
+    Y.wait_ge(sem.vv, v_zero)
+    for k in range(2):
+        Y.dma_start(T.m[:, 512 * k:512 * (k + 1)], T.xs[:, 4 * TOK:4 * TOK + 512]).then_inc(sem.dl, 16)
+
+    V.wait_ge(sem.gi, g_it)
+    v(V.tensor_scalar(T.hold[:, :], T.it4[:, :], T.pf[:, 2:3], 1.0e9, op.is_le, op.mult))
     v(V.tensor_copy(T.cdown[:, 0:1], T.cdi[:, rank:rank + 1]))
-    v_zero = v(V.memset(T.v[:, :], 0.0))
-    v(V.memset(T.xs[:, 4 * TOK:XW], 0.0))
-    v(V.memset(T.m[:, :], BIG))
-    A.wait_ge(sem.vv, v_zero)
-    a_z = a_(A.activation(T.z[:, :], T.v[:, :], act.Copy))
     V.wait_ge(sem.gi, g_bc)
-    for u in range(ND // 16):
-        v(V.tensor_copy(T.tabl[:, 16 * u:16 * u + 16], T.bc[:, ND + u:2 * ND:ND // 16]))
-        n = v(V.tensor_scalar(T.tabs[:, 16 * u:16 * u + 16], T.bc[:, u:ND:ND // 16], 4.0, None, op.mult))
+    n = v(V.tensor_copy(T.tabl[:, :], T.bc[:, ND:2 * ND].indirect(T.turn[:, :])))
+    v(V.tensor_copy(T.tabs[:, :], T.bc[:, 0:ND].indirect(T.turn[:, :])))
     vneed(n)
-    n = v(V.tensor_scalar(T.tabm[:, :], T.tabl[:, :], 4.0, None, op.mult))
-    V.wait_ge(sem.dq, 16)
-    v(V.quantize_mx(T.wq[:, :], T.wp[:, :], T.qwb[:, :]))
-    vneed(n)
-    vneed(v(V.tensor_tensor(T.tabe[:, :], T.tabs[:, :], T.tabm[:, :], op.add)))
+    v_tab = v(V.tensor_tensor(T.tabe[:, :], T.bc[:, 0:ND].indirect(T.turn[:, :]), T.tabl[:, :], op.add))
 
     def end_of(s):
         return T.cs[:, CD * (s + 1):CD * (s + 1) + 1]
 
-    def places_of(d):
-        return end_of(S) if d == rank else T.cl[:, 2 * d:2 * d + 1]
-
-    first = rank + rank % 2
-    numbers = [T.cdl[:, first:first + 1], T.cdx[:, 0:S - 1], T.cdown[:, 0:1]]
+    numbers = [T.cdl[:, N:N + 1], T.cdl[:, LW + N:LW + N + 1], T.cdx[:, 0:S - 2], T.cdown[:, 0:1]]
+    group = [[k for k, (lo, hi) in enumerate(LISTS) if lo <= s < hi][0] for s in range(N)]
 
     def part(s, lo, hi):
         return (T.h[:, 4 * CAP * s + 16 * lo:4 * CAP * s + 16 * hi],
                 T.xs[:, :].indirect(T.off[:, OW * s + lo:OW * s + hi]))
 
-    at, a_of = {}, {}
+    def starts(k):
+        return 16 + MW * k
+
+    at, landed = {}, set()
+
+    def arrived(Q, name, slots):
+        for s in slots:
+            if s < S and (name, s) not in landed:
+                landed.add((name, s))
+                Q.wait_ge(sem["rq%d" % order[s]], nl)
 
     def work(word):
         k = word[0]
         s = int(word[1:] or 0)
         c, w = slice(CAP * s, CAP * (s + 1)), slice(OW * s, OW * (s + 1))
         if k == "i":
-            b = first + N
-            x = v(V.tensor_copy(T.cdx[:, 0:S - 1], T.cdl[:, b:b + N * (S - 2) + 1:N]))
-        elif k in "lgend":
+            arrived(V, "V", range(*LISTS[2]))
+            x = v(V.tensor_copy(T.cdx[:, 0:S - 2], T.cdl[:, 2 * LW + N:LW * S:LW]))
+        elif k in "ge":
             lo, hi = CD * LISTS[s][0], CD * LISTS[s][1]
-            if k in "lge" and s == 1:
-                vneed(at["i"])
+            need(A, sem.vv, av, at["i"] if s == 2 else v_tab)
+            if s != 2:
+                arrived(A, "A", range(*LISTS[s]))
+            if k == "g":
+                x = a_(A.activation(T.sg[:, lo:hi], T.tabs[:, :].indirect(numbers[s]), act.Copy))
+            else:
+                x = a_(A.activation(T.eg[:, lo + 1:hi + 1], T.tabe[:, :].indirect(numbers[s]), act.Copy))
+        elif k in "lnd":
+            lo, hi = CD * LISTS[s][0], CD * LISTS[s][1]
             if k == "l":
-                x = v(V.tensor_tensor(T.lm[:, lo:hi], T.tabl[:, :].indirect(numbers[s]), T.tri[:, lo:hi], op.mult))
-            elif k == "g":
-                x = v(V.tensor_copy(T.sg[:, lo:hi], T.tabs[:, :].indirect(numbers[s])))
-            elif k == "e":
-                x = v(V.tensor_copy(T.eg[:, lo + 1:hi + 1], T.tabe[:, :].indirect(numbers[s])))
+                arrived(V, "V", range(*LISTS[s]))
+                vneed(at.get("i", 0) if s == 2 else 0)
+                x = v(V.tensor_tensor(T.lm[:, lo:hi], T.tabl[:, :].indirect(numbers[s]), T.tri[:, 0:hi - lo], op.mult))
             elif k == "n":
                 vneed(at["l%d" % s])
-                x = v(V.tensor_tensor_scan(T.cs[:, lo + 1:hi + 1], T.rst[:, lo:hi], T.lm[:, lo:hi], 0.0,
+                x = v(V.tensor_tensor_scan(T.cs[:, lo + 1:hi + 1], T.rst[:, 0:hi - lo], T.lm[:, lo:hi], 0.0,
                                            op.mult, op.add))
             else:
-                vneed(max(at["g%d" % s], at["e%d" % s]))
+                need(V, sem.aa, va, max(at["g%d" % s], at["e%d" % s]))
                 x = v(V.tensor_tensor(T.dg[:, lo + 1:hi], T.sg[:, lo + 1:hi], T.eg[:, lo + 1:hi], op.subtract))
+        elif k == "o":
+            vneed(at["n3"])
+            x = v(V.tensor_copy(T.cl[:, 8 * rank:8 * rank + 1], end_of(S)))
         elif k == "s":
-            b = 0 if s == 0 else 2 if s == S else 1
-            vneed(max(at["n%d" % b], at["d%d" % b]))
+            vneed(max(at["n%d" % group[s]], at["d%d" % group[s]]))
             x = v(V.tensor_copy(T.v[:, VW * s:VW * (s + 1)].indirect(end_of(s)), T.dg[:, CD * s + 1:CD * (s + 1) + 1]))
         elif k == "p":
             vneed(at["s%d" % s])
@@ -233,88 +309,126 @@ def rank_program(g, core, T, topo):
             x = v(V.tensor_tensor_scan(T.a[:, c], T.hold[:, :], T.f[:, c], 0.0, op.max, op.min))
         elif k == "c":
             vneed(at["h%d" % s])
-            x = v(V.tensor_scalar(T.off[:, w], T.a[:, CAP * s + 3:CAP * (s + 1):4], T.pf[:, 3:4], None, op.subtract))
-            A.wait_ge(sem.vv, x)
-            o, i = part(s, 0, CUT[s])
-            a_of[s] = a_(A.activation(o, i, act.Copy))
+            x = v(V.tensor_scalar(T.off[:, w], T.a[:, CAP * s + 3:CAP * (s + 1):4], 4.0, T.pf[:, 3:4],
+                                  op.mult, op.subtract))
+        elif k in "ab":
+            if "x" not in landed:
+                landed.add("x")
+                A.wait_ge(sem.dx, 16)
+            need(A, sem.vv, av, at["c%d" % s])
+            o, i = part(s, 0, OWN) if k == "b" else part(s, OWN if s == S else 0, CUT[s])
+            x = a_(A.activation(o, i, act.Copy))
         elif k == "v":
+            if "xv" not in landed:
+                landed.add("xv")
+                V.wait_ge(sem.dx, 16)
             vneed(at["c%d" % s])
             o, i = part(s, CUT[s], OW)
             x = v(V.tensor_copy(o, i))
         elif k == "q":
-            V.wait_ge(sem.aa, a_of[s])
+            need(V, sem.aa, va, at["a%d" % s])
             vneed(at.get("v%d" % s, 0))
             x = v(V.quantize_mx(T.q[:, c], T.p[:, c], T.h[:, 4 * CAP * s:4 * CAP * (s + 1)]))
+        elif k == "M":
+            x = fill(T.v[:, 2 * VW * s:2 * VW * (s + 1)], 2 * VW, 0.0)
+        elif k == "w":
+            V.wait_ge(sem.dq, 16)
+            x = v(V.quantize_mx(T.wq[:, :], T.wp[:, :], T.qwb[:, :]))
+        elif k == "u":
+            V.wait_ge(sem.cc, ne * (len(ends_by) + len(ENDS)))
+            vneed(at["o"])
+            for b in range(2):
+                x = v(V.tensor_scalar(T.ce[:, b:N:2], T.cl[:, 8 * b:8 * N:16], CAP * b - 1.0, None, op.add))
         else:
-            V.wait_ge(sem.cc, sum(share))
-            for d in range(N):
-                x = v(V.tensor_copy(T.m[:, VW * d:VW * (d + 1)].indirect(places_of(d)), T.neg[:, :]))
+            V.wait_ge(sem.dl, 32)
+            vneed(at["u"])
+            for b in range(N // 2):
+                x = v(V.tensor_copy(T.m[:, starts(b):starts(b) + 2 * CAP].indirect(T.ce[:, 2 * b:2 * b + 2]),
+                                    T.neg[:, :]))
         at[word] = x
 
-    for word in EARLY:
+    for word in EARLY + ORDER:
         work(word)
-    A.wait_ge(sem.dx, 16)
-    V.wait_ge(sem.dx, 16)
-    V.wait_ge(sem.aa, a_z)
-    V.wait_ge(sem.rq, rq_total)
-    for word in ORDER:
-        work(word)
-    vneed(at["m"])
 
-    def single(s, sm, o, i):
-        a = topo.addr(T.cores[order[s]])
-        g.remote_dma(o, i, remote_sem=sm, local_sem=sem.ls, pid=a[1], routing_id=a[0],
-                     dma_engine_mask=topo.mask(core, T.cores[order[s]]))
-        ln_[0] += len(eng[s])
-
-    my_end = T.cl[:, 2 * rank:2 * rank + 1]
-    g.wait_ge(sem.vv, max(at["n0"], at["n1"]))
-    ts = []
-    for s in range(4):
-        es = eng[s][share[s] * s:share[s] * (s + 1)]
-        ts.append(RemoteDMATransfer(dst_ids=[ids[s]], dma_engine_mask=bits(es), remote_sem=sem.cc,
-                                    srcs=[end_of(s)], dsts=[my_end]))
-        ln_[0] += len(es)
-    g.remote_dma_fused(ts, local_sem=sem.ls)
-    single(4, sem.cc, my_end, end_of(4))
-
+    my_end = T.cl[:, 8 * rank:8 * rank + 1]
     land = slice(CAP * rank, CAP * (rank + 1))
-    for s in range(S):
+
+    def ends_via():
+        k = len(near) // len(VIA)
+        g.remote_dma_fused([RemoteDMATransfer(
+            dst_ids=[dst_id(helpers[j], topo)], dma_engine_mask=bits(near[k * j:k * (j + 1)]), remote_sem=sem.he,
+            srcs=[end_of(s)], dsts=[T.hl[:, 0:1]]) for j, s in enumerate(ends_by)], local_sem=sem.ls)
+        ln_[0] += len(near)
+
+    def ends(slots):
+        share = [ne]
+        while len(share) < len(slots):
+            share = sorted(share[1:] + [share[0] // 2] * 2, reverse=True)
+        ts, k = [], 0
+        for s, n in zip(slots, share):
+            ts.append(RemoteDMATransfer(dst_ids=[dst_id(T.cores[order[s]], topo)], dma_engine_mask=bits(far[k:k + n]),
+                                        remote_sem=sem.cc, srcs=[end_of(s)], dsts=[my_end]))
+            k += n
+        g.remote_dma_fused(ts, local_sem=sem.ls)
+        ln_[0] += ne
+
+    def tile(s):
         mine = slice(CAP * s, CAP * (s + 1))
-        g.wait_ge(sem.vv, at["q%d" % s])
-        single(s, sem["co%d" % rank], T.rc[:, land].bitcast(dt.uint8), T.q[:, mine].bitcast(dt.uint8))
-        single(s, sem["pl%d" % rank], T.rp[:, land], T.p[:, mine])
+        for k, name, there, here in (("c", "co%d", T.rc, T.q), ("p", "pl%d", T.rp, T.p)):
+            by = [j for j, words in enumerate(VIA) if k + str(s) in words]
+            if by:
+                to, es, sm, o = helpers[by[0]], near, sem[name % s], here[:, mine]
+            else:
+                to, es, sm, o = T.cores[order[s]], far, sem[name % rank], there[:, land]
+            i = here[:, mine]
+            if k == "c":
+                o, i = o.bitcast(dt.uint8), i.bitcast(dt.uint8)
+            ln_[0] += write(g, T, topo, to, es, sm, o, i)
 
-    t_of = {}
+    jobs = [(max(at["n%d" % group[s]] for s in slots), -1 - k) for k, slots in enumerate(ENDS)]
+    if ends_by:
+        jobs.append((max(at["n%d" % group[s]] for s in ends_by), -9))
+    for n, s in sorted(jobs + [(at["q%d" % s], s) for s in range(S)]):
+        g.wait_ge(sem.vv, n)
+        if s == -9:
+            ends_via()
+        elif s < 0:
+            ends(ENDS[-1 - s])
+        else:
+            tile(s)
 
-    def product(b, cq, cp, k):
-        E.matmul_mx(T.ps[:, 512 * b:512 * b + CAP], T.wq[:, :], T.wp[:, :], cq[:, k:k + CAP], cp[:, k:k + CAP],
+    scanned = {}
+    for s in TURN:
+        d = rank if s == S else src[s]
+        if s == TURN[OWN_AT]:
+            work("q%d" % S)
+        if s == S:
+            E.wait_ge(sem.vv, at["q%d" % S])
+            cq, cp, k = T.q, T.p, CAP * S
+        else:
+            if not tn[0]:
+                E.wait_ge(sem.vv, at["w"])
+            E.wait_ge(sem["co%d" % d], ne)
+            E.wait_ge(sem["pl%d" % d], ne)
+            cq, cp, k = T.rc, T.rp, CAP * d
+        E.matmul_mx(T.ps[:, 512 * d:512 * d + CAP], T.wq[:, :], T.wp[:, :], cq[:, k:k + CAP], cp[:, k:k + CAP],
                     True, True).then_inc(sem.tt, 1)
         tn[0] += 1
-        t_of[b] = tn[0]
-    turn = src[:OWN_AT] + [rank] + src[OWN_AT:]
-    for d in turn:
-        if d == rank:
-            E.wait_ge(sem.vv, at["q%d" % S])
-            product(rank, T.q, T.p, CAP * S)
-        else:
-            if not t_of:
-                E.wait_ge(sem.vv, at["q0"])
-            E.wait_ge(sem["co%d" % d], len(topo.engines(T.cores[d], core)))
-            E.wait_ge(sem["pl%d" % d], len(topo.engines(T.cores[d], core)))
-            product(d, T.rc, T.rp, CAP * d)
-
-    for d in turn:
-        V.wait_ge(sem.tt, t_of[d])
-        n = v(V.tensor_tensor_scan(T.z[:, VW * d + 1:VW * d + CAP + 1], T.m[:, VW * d:VW * d + CAP],
-                                   T.ps[:, 512 * d:512 * d + CAP], -BIG, op.min, op.max))
-        o, i = T.ys[:, CD * d:CD * (d + 1)], T.z[:, VW * d:VW * (d + 1)].indirect(places_of(d))
-        if d != turn[-1]:
-            A.wait_ge(sem.vv, n)
-            a_(A.activation(o, i, act.Copy))
-        else:
-            vneed(n)
-            n = v(V.tensor_copy(o, i))
+        vneed(at["m"])
+        V.wait_ge(sem.tt, tn[0])
+        b = starts(d // 2) + CAP * (d % 2) - 1
+        n = v(V.tensor_tensor_scan(T.z[:, CAP * d:CAP * (d + 1)], T.m[:, b:b + CAP],
+                                   T.ps[:, 512 * d:512 * d + CAP], -BIG, op.add, op.max))
+        scanned[d] = n
+        b = d - d % 2
+        if b in scanned and b + 1 in scanned:
+            o, i = T.ys[:, CD * b:CD * (b + 2)], T.z[:, CAP * b:CAP * (b + 2)].indirect(T.ce[:, b:b + 2])
+            if s != TURN[-1]:
+                need(A, sem.vv, av, n)
+                a_(A.activation(o, i, act.Copy))
+            else:
+                vneed(n)
+                n = v(V.tensor_copy(o, i))
     Y.wait_ge(sem.aa, an[0])
     Y.wait_ge(sem.vv, n)
     Y.dma_start(T.y[:, :], T.ys[:, :]).then_inc(sem.dy, 16)

@@ -1,58 +1,59 @@
-import numpy as np
 from concourse.bass import DstId, RemoteDMATransfer
 from concourse.mybir import dt, AluOpType, ActivationFunctionType
 
 N, CD, ND, TOK, CAP = 6, 16, 64, 768, 160
 S = N - 1
+R = 4
+ROW = [0, 1, 1, 2, 2, 3]
+HALF = [None, 0, 1, 0, 1, None]
+PICKS = {S: (0, 0, 2), 3: (2, 2, 3), 2: (2, 3, 5)}
+PLACE = [1, 4, 3, 2, 5, 0]
+LO, HI = slice(0, 64), slice(64, 128)
 VW = CAP + 8
 XW = 4 * (TOK + CAP)
 OW = 4 * CAP // 16
 MW = 2 * CAP + 16
 LW = 2 * N
-XA = 4 * TOK
+XA = 4 * TOK - 512
 RAMP = 1024
 BIG = 1.0e29
-LISTS = [(0, 1), (1, 2), (2, S), (S, N)]
-CUT = [40, 24, 40, 24, 22, 40]
-ENDS = [[1, 2, 3, 4]]
-OWN_AT = 0
-VIA = [["e0", "c0", "p0"]]
-TURN = [1, 2, S, 0, 3, 4]
-OWN = 8
-EARLY = "M2 M1 l3 g3 e3 n3 d3 o s5 p5 h5 c5".split()
-ORDER = ("g0 e0 l0 g1 e1 l1 n0 n1 d0 i g2 e2 b5 s0 d1 l2 p0 s1 h0 d2 c0 a0 n2 p1 s2 s3 s4 h1 p2 c1 a1 p3 h2 p4 c2 a2 "
-         "q0 h3 v1 h4 c3 a3 q1 c4 a4 a5 v3 q2 v4 q3 u w q4 m").split()
+CUT = [34, 36, 16, 24, 28, 28]
+VIA = [["e0", "h0", "p0", "h1", "p1", "p2"]]
+ENDS = [1, 2, 3, 4]
+TURN = [0, S, 3, 1, 2, 4]
+ORDER = ("l0 e0 n0 d0 i g1 e1 s0 l1 p0 n1 d1 h0 c0 a0 s1 s2 s3 p1 v0 h1 p2 c1 a1 c2 a2 h2 v1 q0 c3 a3 v2 q1 c4 a4 q2 "
+         "v3 p3 q3 h3 v4 c5 a5 q4 v5 u q5 m").split()
 
 SCRATCH = {
     "cdi": ("sbuf", [128, N], "int32"),
-    "cdu": ("sbuf", [128, N], "uint16"),
+    "cdu": ("sbuf", [128, N + 2], "uint16"),
     "cdl": ("sbuf", [128, LW * S], "uint16"),
     "cdx": ("sbuf", [128, 4], "uint16"),
-    "cdown": ("sbuf", [128, 2], "uint16"),
     "raw": ("sbuf", [128, 2 * ND], "int32"),
-    "bc": ("sbuf", [128, 2 * ND], "int32"),
-    "tabs": ("sbuf", [128, ND], "float32"),
+    "bc": ("sbuf", [128, ND], "int32"),
+    "one": ("sbuf", [128, ND], "float32"),
+    "tab": ("sbuf", [128, 2 * ND], "float32"),
     "tabl": ("sbuf", [128, ND], "float32"),
-    "tabe": ("sbuf", [128, ND], "float32"),
     "ip": ("sbuf", [128, 4], "int32"),
     "ii": ("sbuf", [128, 8], "int32"),
     "turn": ("sbuf", [128, 4], "uint16"),
     "pf": ("sbuf", [128, 4], "float32"),
-    "it16": ("sbuf", [128, 4 * CD], "float32"),
-    "it4": ("sbuf", [128, CAP], "float32"),
-    "tri": ("sbuf", [128, 4 * CD], "float32"),
-    "rst": ("sbuf", [128, 4 * CD], "float32"),
+    "it16": ("sbuf", [128, 2 * CD], "float32"),
+    "hb": ("sbuf", [128, 4], "float32"),
+    "tri": ("sbuf", [128, 2 * CD], "float32"),
+    "rst": ("sbuf", [128, 2 * CD], "float32"),
     "hold": ("sbuf", [128, CAP], "bfloat16"),
     "inc": ("sbuf", [128, CAP], "float32"),
-    "neg": ("sbuf", [128, 2 * CD], "bfloat16"),
-    "lm": ("sbuf", [128, N * CD], "float32"),
-    "cs": ("sbuf", [128, N * CD + 8], "uint16"),
-    "sg": ("sbuf", [128, N * CD], "float32"),
-    "eg": ("sbuf", [128, N * CD + 8], "float32"),
-    "dg": ("sbuf", [128, N * CD + 8], "float32"),
-    "v": ("sbuf", [128, N * VW], "float32"),
-    "f": ("sbuf", [128, N * CAP], "uint16"),
-    "a": ("sbuf", [128, N * CAP], "uint16"),
+    "neg": ("sbuf", [128, N * CD], "bfloat16"),
+    "base": ("sbuf", [128, N], "float32"),
+    "lm": ("sbuf", [128, R * CD], "float32"),
+    "cs": ("sbuf", [128, R * CD + 8], "uint16"),
+    "sg": ("sbuf", [128, R * CD], "float32"),
+    "eg": ("sbuf", [128, R * CD + 8], "float32"),
+    "dg": ("sbuf", [128, R * CD + 8], "float32"),
+    "v": ("sbuf", [128, R * VW], "float32"),
+    "f": ("sbuf", [128, R * CAP], "uint16"),
+    "a": ("sbuf", [128, R * CAP], "uint16"),
     "off": ("sbuf", [128, N * OW], "uint16"),
     "xs": ("sbuf", [128, XW], "bfloat16"),
     "h": ("sbuf", [128, N * 4 * CAP], "bfloat16"),
@@ -69,9 +70,10 @@ SCRATCH = {
     "m": ("sbuf", [128, 16 + MW * (N // 2)], "bfloat16"),
     "z": ("sbuf", [128, N * CAP], "float32"),
     "ys": ("sbuf", [128, N * CD], "float32"),
+    "yo": ("sbuf", [128, 2 * CD], "float32"),
     "ps": ("psum", [128, 512 * N], "float32"),
 }
-SEMAPHORES = ["dc", "dr", "dx", "dq", "dy", "gi", "vv", "aa", "tt", "ls", "ll", "cc", "he", "dl"] \
+SEMAPHORES = ["dc", "dn", "dr", "dx", "dq", "dl", "dy", "gi", "vv", "aa", "tt", "ls", "ll", "cc", "he", "go"] \
     + [k + str(i) for k in ("rq", "co", "pl") for i in range(N)]
 
 
@@ -87,8 +89,11 @@ def order_of(r, T, topo):
 
 
 def helpers_of(r, T, topo):
-    c = T.cores[r]
-    return [h for h in topo.cores_of(c) if topo.die(h) != topo.die(c) and all(topo.may_write(h, d) for d in T.cores)]
+    c, order, found = T.cores[r], order_of(r, T, topo), []
+    for words in VIA:
+        found.append([h for h in topo.cores_of(c) if h not in found and topo.die(h) != topo.die(c)
+                      and all(topo.may_write(h, T.cores[order[int(w[1])]]) for w in words)][0])
+    return found
 
 
 def bits(es):
@@ -110,26 +115,33 @@ def spare(core, to, far, topo):
     return [e for e in topo.engines(core, to) if e not in topo.engines(core, far)]
 
 
+def codes(buf, lo, hi):
+    return buf[:, lo:hi].bitcast(dt.uint8)
+
+
+def ends_at(T, s):
+    return T.cl[:, 8 * PLACE[s]:8 * PLACE[s] + 1]
+
+
 def helper_program(g, core, r, k, T, topo):
     order = order_of(r, T, topo)
-    land = slice(CAP * r, CAP * (r + 1))
     n = 0
     for word in VIA[k]:
         s = int(word[1])
         to = T.cores[order[s]]
         es = topo.engines(core, to)
         ne = len(spare(T.cores[r], core, to, topo))
-        mine = slice(CAP * s, CAP * (s + 1))
+        lo, hi = CAP * s, CAP * (s + 1)
         if word[0] == "e":
             g.wait_ge(T.sem.he, ne // len(VIA))
-            n += write(g, T, topo, to, es, T.sem.cc, T.cl[:, 8 * r:8 * r + 1], T.hl[:, 0:1])
-        elif word[0] == "c":
+            n += write(g, T, topo, to, es, T.sem.cc, ends_at(T, s), T.hl[:, 0:1])
+        elif word[0] == "h":
             g.wait_ge(T.sem["co%d" % s], ne)
-            n += write(g, T, topo, to, es, T.sem["co%d" % r], T.rc[:, land].bitcast(dt.uint8),
-                       T.q[:, mine].bitcast(dt.uint8))
+            n += write(g, T, topo, to, es, T.sem["co%d" % s], codes(T.rc, lo + CAP // 2, hi),
+                       codes(T.q, lo + CAP // 2, hi))
         else:
             g.wait_ge(T.sem["pl%d" % s], ne)
-            n += write(g, T, topo, to, es, T.sem["pl%d" % r], T.rp[:, land], T.p[:, mine])
+            n += write(g, T, topo, to, es, T.sem["pl%d" % s], T.rp[:, lo:hi], T.p[:, lo:hi])
     g.wait_ge(T.sem.ls, n)
 
 
@@ -137,7 +149,7 @@ def rank_program(g, core, T, topo):
     rank = T.rank_of(core)
     if rank is None:
         for r in range(N):
-            hs = helpers_of(r, T, topo)[:len(VIA)]
+            hs = helpers_of(r, T, topo)
             if core in hs:
                 helper_program(g, core, r, hs.index(core), T, topo)
         return
@@ -148,12 +160,12 @@ def rank_program(g, core, T, topo):
     order = orders[rank]
     src = [[r for r in range(N) if r != rank and orders[r][s] == rank][0] for s in range(S)]
     helpers = helpers_of(rank, T, topo)
+    by = {word: helpers[k] for k, words in enumerate(VIA) for word in words}
     far = topo.engines(core, T.cores[order[0]])
     near = spare(core, helpers[0], T.cores[order[0]], topo)
     ne = len(far)
-    ends_by = [int(words[0][1]) for words in VIA if words[0][0] == "e"]
 
-    vn, vw, an, aw, av, va, tn, gn, ln_ = [0], [0], [0], [0], [0], [0], [0], [0], [0]
+    vn, vw, an, av, va, tn, gn, sent = [0], [0], [0], [0], [0], [0], [0], [0]
 
     def v(ins):
         ins.then_inc(sem.vv, 1)
@@ -165,6 +177,11 @@ def rank_program(g, core, T, topo):
         an[0] += 1
         return an[0]
 
+    def gi(ins):
+        ins.then_inc(sem.gi, 1)
+        gn[0] += 1
+        return gn[0]
+
     def need(Q, sm, seen, n):
         if n > seen[0]:
             Q.wait_ge(sm, n)
@@ -173,20 +190,16 @@ def rank_program(g, core, T, topo):
     def vneed(n):
         need(V, sem.vv, vw, n)
 
-    def gi(ins):
-        ins.then_inc(sem.gi, 1)
-        gn[0] += 1
-        return gn[0]
-
-    A.dma_start(T.raw[0:1, ND:2 * ND], T.ln[:, :]).then_inc(sem.dr, 16)
-    Y.dma_start(T.raw[0:1, 0:ND], T.st[:, :]).then_inc(sem.dr, 16)
-    for k in range(8):
+    A.dma_start(T.raw[0:1, ND:2 * ND], T.ln[:, :]).then_inc(sem.dn, 16)
+    for k in range(4):
         (Y if k % 2 == 0 else A).dma_start(T.cdi[16 * k:16 * k + 16, 0:N], T.cd[:, :]).then_inc(sem.dc, 16)
+    Y.dma_start(T.raw[0:1, 0:ND], T.st[:, :]).then_inc(sem.dr, 16)
+    A.dma_start(T.qwb[:, :], T.qw[:, :]).then_inc(sem.dq, 16)
     Y.dma_start(T.xs[:, 0:XA], T.x[:, 0:XA]).then_inc(sem.dx, 16)
 
     g_ip = gi(g.iota(T.ip[:, :], [[1, 4]], 0, 4))
-    gi(g.iota(T.it16[:, :], [[0, 4], [1, CD]], 0, 0, allow_small_or_imprecise_dtypes=True))
-    g_it = gi(g.iota(T.it4[:, :], [[0, CAP // 4], [1, 4]], 0, 0, allow_small_or_imprecise_dtypes=True))
+    g_it = gi(g.iota(T.it16[:, :], [[0, 2], [1, CD]], 0, 0, allow_small_or_imprecise_dtypes=True))
+    gi(g.iota(T.base[:, :], [[CAP, N]], -1, 0, allow_small_or_imprecise_dtypes=True))
 
     v_zero = v(V.memset(T.xs[:, 4 * TOK:XW], 0.0))
     V.wait_ge(sem.gi, g_ip)
@@ -195,60 +208,68 @@ def rank_program(g, core, T, topo):
     v(V.tensor_scalar(T.ii[:, 2:3], T.ip[:, 0:1], 4, 3, op.logical_shift_right, op.bitwise_and))
     n = v(V.tensor_scalar(T.ii[:, 4:8], T.ip[:, :], ND - 1, None, op.bitwise_and))
     v(V.memset(T.dg[:, :], 0.0))
-    v(V.memset(T.neg[:, :], -BIG))
     vneed(n)
     n = v(V.tensor_copy(T.pf[:, 0:3], T.ii[:, 0:3]))
     v(V.tensor_copy(T.turn[:, :], T.ii[:, 4:8]))
-    V.wait_ge(sem.gi, g_ip + 1)
+    V.wait_ge(sem.gi, g_it)
     v(V.tensor_scalar(T.rst[:, :], T.it16[:, :], 1.0, None, op.min))
     vneed(n + 1)
-    v(V.tensor_scalar(T.tri[:, :], T.it16[:, :], T.pf[:, 0:1], None, op.is_le))
-    v(V.tensor_scalar(T.pf[:, 3:4], T.pf[:, 2:3], 4.0 * RAMP, T.pf[:, 1:2], op.mult, op.subtract))
-
-    need(A, sem.vv, av, v_zero)
+    v_hb = v(V.tensor_scalar(T.hb[:, :], T.it16[:, 0:4], T.pf[:, 2:3], 1.0e9, op.is_le, op.mult))
 
     def fill(o, n, c):
         i = T.xs[:, 4 * TOK:4 * TOK + n]
-        return a_(A.activation(o, i, act.Identity, bias=c) if c else A.activation(o, i, act.Copy))
-    fill(T.v[:, 0:2 * VW], 2 * VW, 0.0)
-    fill(T.inc[:, 0:1], 1, 0.0)
+        return a_(A.activation(o, i, act.Copy) if c is None else A.activation(o, i, act.Identity, bias=c))
+    need(A, sem.vv, av, v_zero)
+    for k in range(2):
+        fill(T.v[:, 2 * VW * k:2 * VW * (k + 1)], 2 * VW, None)
+    fill(T.inc[:, 0:1], 1, None)
     fill(T.inc[:, 4:CAP:4], CAP // 4 - 1, 1.0 - 3 * RAMP)
     for u in range(1, 4):
-        a_inc = fill(T.inc[:, u:CAP:4], CAP // 4, 1.0 + RAMP)
+        fill(T.inc[:, u:CAP:4], CAP // 4, 1.0 + RAMP)
+    need(A, sem.vv, av, v_hb)
+    for u in range(4):
+        fill(T.hold[:, u:CAP:4], CAP // 4, T.hb[:, u:u + 1])
+    fill(T.eg[:, 0:1], 1, None)
+    a_fill = fill(T.neg[:, :], N * CD, -BIG)
 
-    g.wait_ge(sem.dr, 32)
-    g_bc = gi(g.partition_broadcast(T.bc[:, :], T.raw[0:1, :], 128))
+    g.wait_ge(sem.dn, 16)
+    g_bl = gi(g.partition_broadcast(T.bc[:, :], T.raw[0:1, ND:2 * ND], 128))
 
-    V.wait_ge(sem.dc, 128)
-    v_cdu = v(V.tensor_copy(T.cdu[:, :], T.cdi[:, :]))
+    V.wait_ge(sem.dc, 64)
+    o = rank % 2
+    for half in (LO, HI):
+        v_cdu = v(V.tensor_copy(T.cdu[half, o:o + N], T.cdi[LO, :]))
     g.wait_ge(sem.vv, v_cdu)
-    at_d = [LW * s + N - d for s, d in enumerate(src)]
-    nl = ne
-    for lo, hi, es in ((0, S, far),):
-        g.remote_dma_fused([RemoteDMATransfer(
-            dst_ids=[dst_id(T.cores[d], topo) for d in src[lo:hi]], dma_engine_mask=bits(es),
-            remote_sem=sem["rq%d" % rank], srcs=[T.cdu[:, :]], dsts=[T.cdl[:, b:b + N] for b in at_d[lo:hi]])],
-            local_sem=sem.ll)
+    g.remote_dma_fused([RemoteDMATransfer(
+        dst_ids=[dst_id(T.cores[d], topo) for d in src], dma_engine_mask=bits(far), remote_sem=sem["rq%d" % rank],
+        srcs=[T.cdu[:, o:o + N]], dsts=[T.cdl[:, LW * s + N - d:LW * s + 2 * N - d] for s, d in enumerate(src)])],
+        local_sem=sem.ll)
+    g.sem_inc(sem.go, 1)
+    Y.wait_ge(sem.go, 1)
+    Y.dma_start(T.xs[:, XA:4 * TOK], T.x[:, XA:4 * TOK]).then_inc(sem.dx, 16)
     Y.wait_ge(sem.ll, ne)
-    Y.dma_start(T.qwb[:, :], T.qw[:, :]).then_inc(sem.dq, 16)
     Y.wait_ge(sem.vv, v_zero)
     for k in range(2):
         Y.dma_start(T.m[:, 512 * k:512 * (k + 1)], T.xs[:, 4 * TOK:4 * TOK + 512]).then_inc(sem.dl, 16)
 
-    V.wait_ge(sem.gi, g_it)
-    v(V.tensor_scalar(T.hold[:, :], T.it4[:, :], T.pf[:, 2:3], 1.0e9, op.is_le, op.mult))
-    v(V.tensor_copy(T.cdown[:, 0:1], T.cdi[:, rank:rank + 1]))
-    V.wait_ge(sem.gi, g_bc)
-    n = v(V.tensor_copy(T.tabl[:, :], T.bc[:, ND:2 * ND].indirect(T.turn[:, :])))
-    v(V.tensor_copy(T.tabs[:, :], T.bc[:, 0:ND].indirect(T.turn[:, :])))
+    V.wait_ge(sem.dr, 16)
+    for u in range(ND // 16):
+        n = v(V.tensor_copy(T.one[0:1, 16 * u:16 * (u + 1)], T.raw[0:1, u:ND:ND // 16]))
+    g.wait_ge(sem.vv, n)
+    g_bs = gi(g.partition_broadcast(T.tab[:, 0:ND], T.one[0:1, :], 128))
+    V.wait_ge(sem.gi, g_bl)
+    v(V.tensor_copy(T.tabl[:, :], T.bc[:, :].indirect(T.turn[:, :])))
+    n = v(V.tensor_scalar(T.tri[:, :], T.it16[:, :], T.pf[:, 0:1], None, op.is_le))
+    v(V.tensor_scalar(T.pf[:, 3:4], T.pf[:, 2:3], -4.0 * RAMP, T.pf[:, 1:2], op.mult, op.add))
     vneed(n)
-    v_tab = v(V.tensor_tensor(T.tabe[:, :], T.bc[:, 0:ND].indirect(T.turn[:, :]), T.tabl[:, :], op.add))
+    A.wait_ge(sem.gi, g_bs)
 
-    def end_of(s):
-        return T.cs[:, CD * (s + 1):CD * (s + 1) + 1]
+    own = T.cdu[:, rank + o:rank + o + 1]
+    lengths = {0: (0, 1, T.cdl[:, N:N + 1]), 1: (1, 3, T.cdx[:, 0:2]), 3: (3, 4, own)}
+    columns = {0: (0, 1, T.cdl[:, N:N + 1]), 1: (1, 4, T.cdx[:, 0:3])}
 
-    numbers = [T.cdl[:, N:N + 1], T.cdl[:, LW + N:LW + N + 1], T.cdx[:, 0:S - 2], T.cdown[:, 0:1]]
-    group = [[k for k, (lo, hi) in enumerate(LISTS) if lo <= s < hi][0] for s in range(N)]
+    def end_of(r):
+        return T.cs[:, CD * (r + 1):CD * (r + 1) + 1]
 
     def part(s, lo, hi):
         return (T.h[:, 4 * CAP * s + 16 * lo:4 * CAP * s + 16 * hi],
@@ -257,180 +278,183 @@ def rank_program(g, core, T, topo):
     def starts(k):
         return 16 + MW * k
 
-    at, landed = {}, set()
+    at, waited = {}, set()
 
-    def arrived(Q, name, slots):
-        for s in slots:
-            if s < S and (name, s) not in landed:
-                landed.add((name, s))
-                Q.wait_ge(sem["rq%d" % order[s]], nl)
+    def once(Q, name, sm, n):
+        if (name, sm) not in waited:
+            waited.add((name, sm))
+            Q.wait_ge(sem[sm], n)
 
     def work(word):
         k = word[0]
         s = int(word[1:] or 0)
-        c, w = slice(CAP * s, CAP * (s + 1)), slice(OW * s, OW * (s + 1))
+        c = slice(CAP * s, CAP * (s + 1))
         if k == "i":
-            arrived(V, "V", range(*LISTS[2]))
-            x = v(V.tensor_copy(T.cdx[:, 0:S - 2], T.cdl[:, 2 * LW + N:LW * S:LW]))
+            for t in range(1, S):
+                A.wait_ge(sem["rq%d" % order[t]], ne)
+            for b, half in enumerate((LO, HI)):
+                x = a_(A.activation(T.cdx[half, 0:2], T.cdl[half, LW * (1 + b) + N:LW * S:2 * LW], act.Copy))
+            A.wait_ge(sem.aa, x)
+            need(A, sem.vv, av, at["tab"])
+        elif word == "e0":
+            vneed(at["tab"])
+            x = v(V.tensor_copy(T.eg[:, 1:CD + 1], T.tab[:, ND:2 * ND].indirect(columns[0][2])))
+        elif word == "d0":
+            need(V, sem.aa, va, a_fill)
+            vneed(at["e0"])
+            x = v(V.tensor_tensor(T.dg[:, 0:CD], T.tab[:, 0:ND].indirect(columns[0][2]), T.eg[:, 0:CD], op.subtract))
         elif k in "ge":
-            lo, hi = CD * LISTS[s][0], CD * LISTS[s][1]
-            need(A, sem.vv, av, at["i"] if s == 2 else v_tab)
-            if s != 2:
-                arrived(A, "A", range(*LISTS[s]))
+            lo, hi, numbers = columns[s]
+            lo, hi = CD * lo, CD * hi
             if k == "g":
-                x = a_(A.activation(T.sg[:, lo:hi], T.tabs[:, :].indirect(numbers[s]), act.Copy))
+                x = a_(A.activation(T.sg[:, lo:hi], T.tab[:, 0:ND].indirect(numbers), act.Copy))
             else:
-                x = a_(A.activation(T.eg[:, lo + 1:hi + 1], T.tabe[:, :].indirect(numbers[s]), act.Copy))
-        elif k in "lnd":
-            lo, hi = CD * LISTS[s][0], CD * LISTS[s][1]
+                x = a_(A.activation(T.eg[:, lo + 1:hi + 1], T.tab[:, ND:2 * ND].indirect(numbers), act.Copy))
+        elif k in "ln":
+            lo, hi, numbers = lengths[s]
+            lo, hi = CD * lo, CD * hi
             if k == "l":
-                arrived(V, "V", range(*LISTS[s]))
-                vneed(at.get("i", 0) if s == 2 else 0)
-                x = v(V.tensor_tensor(T.lm[:, lo:hi], T.tabl[:, :].indirect(numbers[s]), T.tri[:, 0:hi - lo], op.mult))
-            elif k == "n":
+                need(V, sem.aa, va, at["i"] if s == 1 else 0)
+                x = v(V.tensor_tensor(T.lm[:, lo:hi], T.tabl[:, :].indirect(numbers), T.tri[:, 0:hi - lo], op.mult))
+            else:
                 vneed(at["l%d" % s])
                 x = v(V.tensor_tensor_scan(T.cs[:, lo + 1:hi + 1], T.rst[:, 0:hi - lo], T.lm[:, lo:hi], 0.0,
                                            op.mult, op.add))
-            else:
-                need(V, sem.aa, va, max(at["g%d" % s], at["e%d" % s]))
-                x = v(V.tensor_tensor(T.dg[:, lo + 1:hi], T.sg[:, lo + 1:hi], T.eg[:, lo + 1:hi], op.subtract))
-        elif k == "o":
-            vneed(at["n3"])
-            x = v(V.tensor_copy(T.cl[:, 8 * rank:8 * rank + 1], end_of(S)))
+        elif k == "d":
+            lo, hi = CD * columns[s][0], CD * columns[s][1]
+            need(V, sem.aa, va, max(at["g%d" % s], at["e%d" % s]))
+            x = v(V.tensor_tensor(T.dg[:, lo + 1:hi], T.sg[:, lo + 1:hi], T.eg[:, lo + 1:hi], op.subtract))
         elif k == "s":
-            vneed(max(at["n%d" % group[s]], at["d%d" % group[s]]))
+            need(V, sem.aa, va, a_fill)
+            vneed(max(at["n%d" % min(s, 1)], at["d%d" % min(s, 1)]))
             x = v(V.tensor_copy(T.v[:, VW * s:VW * (s + 1)].indirect(end_of(s)), T.dg[:, CD * s + 1:CD * (s + 1) + 1]))
         elif k == "p":
+            need(V, sem.aa, va, a_fill)
             vneed(at["s%d" % s])
             x = v(V.tensor_tensor_scan(T.f[:, c], T.inc[:, :], T.v[:, VW * s:VW * s + CAP],
-                                       T.sg[:, CD * s:CD * s + 1], op.add, op.add))
+                                       (T.sg if s else T.dg)[:, CD * s:CD * s + 1], op.add, op.add))
         elif k == "h":
             vneed(at["p%d" % s])
             x = v(V.tensor_tensor_scan(T.a[:, c], T.hold[:, :], T.f[:, c], 0.0, op.max, op.min))
+        elif k == "c" and HALF[s] is None:
+            r = ROW[s]
+            need(A, sem.vv, av, at["h%d" % r])
+            x = a_(A.activation(T.off[:, OW * s:OW * (s + 1)], T.a[:, CAP * r + 3:CAP * (r + 1):4], act.Identity,
+                                bias=T.pf[:, 3:4], scale=4.0))
+            A.wait_ge(sem.aa, x)
         elif k == "c":
-            vneed(at["h%d" % s])
-            x = v(V.tensor_scalar(T.off[:, w], T.a[:, CAP * s + 3:CAP * (s + 1):4], 4.0, T.pf[:, 3:4],
-                                  op.mult, op.subtract))
-        elif k in "ab":
-            if "x" not in landed:
-                landed.add("x")
-                A.wait_ge(sem.dx, 16)
-            need(A, sem.vv, av, at["c%d" % s])
-            o, i = part(s, 0, OWN) if k == "b" else part(s, OWN if s == S else 0, CUT[s])
-            x = a_(A.activation(o, i, act.Copy))
+            r, both = ROW[s], slice(0, 128)
+            vneed(at["h%d" % r])
+            moves = [(both, both)] if HALF[s] is None else [(to, (LO, HI)[HALF[s]]) for to in (LO, HI)]
+            for to, of in moves:
+                x = v(V.tensor_scalar(T.off[to, OW * s:OW * (s + 1)], T.a[of, CAP * r + 3:CAP * (r + 1):4], 4.0,
+                                      T.pf[of, 3:4], op.mult, op.add))
+        elif k == "a":
+            once(A, "A", "dx", 32)
+            if HALF[s] is not None:
+                need(A, sem.vv, av, at["c%d" % s])
+            x = a_(A.activation(*part(s, 0, CUT[s]), act.Copy))
         elif k == "v":
-            if "xv" not in landed:
-                landed.add("xv")
-                V.wait_ge(sem.dx, 16)
-            vneed(at["c%d" % s])
-            o, i = part(s, CUT[s], OW)
-            x = v(V.tensor_copy(o, i))
+            once(V, "V", "dx", 32)
+            if HALF[s] is None:
+                need(V, sem.aa, va, at["c%d" % s])
+            else:
+                vneed(at["c%d" % s])
+            x = v(V.tensor_copy(*part(s, CUT[s], OW)))
         elif k == "q":
             need(V, sem.aa, va, at["a%d" % s])
             vneed(at.get("v%d" % s, 0))
             x = v(V.quantize_mx(T.q[:, c], T.p[:, c], T.h[:, 4 * CAP * s:4 * CAP * (s + 1)]))
-        elif k == "M":
-            x = fill(T.v[:, 2 * VW * s:2 * VW * (s + 1)], 2 * VW, 0.0)
         elif k == "w":
             V.wait_ge(sem.dq, 16)
             x = v(V.quantize_mx(T.wq[:, :], T.wp[:, :], T.qwb[:, :]))
         elif k == "u":
-            V.wait_ge(sem.cc, ne * (len(ends_by) + len(ENDS)))
-            vneed(at["o"])
-            for b in range(2):
-                x = v(V.tensor_scalar(T.ce[:, b:N:2], T.cl[:, 8 * b:8 * N:16], CAP * b - 1.0, None, op.add))
+            V.wait_ge(sem.cc, ne * (len(VIA) + 1))
+            for b, of in enumerate((LO, HI)):
+                for to in (LO, HI):
+                    x = v(V.tensor_tensor(T.ce[to, b:N:2], T.cl[of, 8 * b:8 * N:16], T.base[of, b:N:2], op.add))
         else:
             V.wait_ge(sem.dl, 32)
             vneed(at["u"])
-            for b in range(N // 2):
-                x = v(V.tensor_copy(T.m[:, starts(b):starts(b) + 2 * CAP].indirect(T.ce[:, 2 * b:2 * b + 2]),
-                                    T.neg[:, :]))
+            x = v(V.tensor_copy(T.m[:, 16:16 + N * CAP].indirect(T.ce[:, :]), T.neg[:, :]))
         at[word] = x
 
-    for word in EARLY + ORDER:
+    work("l3")
+    v(V.tensor_copy(T.cdx[:, 2:3], own))
+    work("n3")
+    work("w")
+    V.wait_ge(sem.gi, g_bs)
+    at["tab"] = v(V.tensor_tensor(T.tab[:, ND:2 * ND], T.tab[:, 0:ND], T.tabl[:, :], op.add))
+    vneed(at["n3"])
+    v(V.tensor_copy(ends_at(T, S), end_of(ROW[S])))
+    V.wait_ge(sem["rq%d" % order[0]], ne)
+    for word in ORDER:
         work(word)
 
-    my_end = T.cl[:, 8 * rank:8 * rank + 1]
-    land = slice(CAP * rank, CAP * (rank + 1))
+    def transfer(to, es, sm, o, i):
+        sent[0] += len(es)
+        return RemoteDMATransfer(dst_ids=[dst_id(to, topo)], dma_engine_mask=bits(es), remote_sem=sm, srcs=[i], dsts=[o])
 
-    def ends_via():
-        k = len(near) // len(VIA)
-        g.remote_dma_fused([RemoteDMATransfer(
-            dst_ids=[dst_id(helpers[j], topo)], dma_engine_mask=bits(near[k * j:k * (j + 1)]), remote_sem=sem.he,
-            srcs=[end_of(s)], dsts=[T.hl[:, 0:1]]) for j, s in enumerate(ends_by)], local_sem=sem.ls)
-        ln_[0] += len(near)
-
-    def ends(slots):
-        share = [ne]
-        while len(share) < len(slots):
-            share = sorted(share[1:] + [share[0] // 2] * 2, reverse=True)
-        ts, k = [], 0
-        for s, n in zip(slots, share):
-            ts.append(RemoteDMATransfer(dst_ids=[dst_id(T.cores[order[s]], topo)], dma_engine_mask=bits(far[k:k + n]),
-                                        remote_sem=sem.cc, srcs=[end_of(s)], dsts=[my_end]))
-            k += n
-        g.remote_dma_fused(ts, local_sem=sem.ls)
-        ln_[0] += ne
-
-    def tile(s):
-        mine = slice(CAP * s, CAP * (s + 1))
-        for k, name, there, here in (("c", "co%d", T.rc, T.q), ("p", "pl%d", T.rp, T.p)):
-            by = [j for j, words in enumerate(VIA) if k + str(s) in words]
-            if by:
-                to, es, sm, o = helpers[by[0]], near, sem[name % s], here[:, mine]
-            else:
-                to, es, sm, o = T.cores[order[s]], far, sem[name % rank], there[:, land]
-            i = here[:, mine]
-            if k == "c":
-                o, i = o.bitcast(dt.uint8), i.bitcast(dt.uint8)
-            ln_[0] += write(g, T, topo, to, es, sm, o, i)
-
-    jobs = [(max(at["n%d" % group[s]] for s in slots), -1 - k) for k, slots in enumerate(ENDS)]
-    if ends_by:
-        jobs.append((max(at["n%d" % group[s]] for s in ends_by), -9))
-    for n, s in sorted(jobs + [(at["q%d" % s], s) for s in range(S)]):
-        g.wait_ge(sem.vv, n)
-        if s == -9:
-            ends_via()
-        elif s < 0:
-            ends(ENDS[-1 - s])
+    g.wait_ge(sem.vv, max(at["n%d" % min(1, int(w[0][1]))] for w in VIA))
+    k = len(near) // len(VIA)
+    g.remote_dma_fused([transfer(helpers[j], near[k * j:k * (j + 1)], sem.he, T.hl[:, 0:1], end_of(ROW[int(w[0][1])]))
+                        for j, w in enumerate(VIA)], local_sem=sem.ls)
+    g.wait_ge(sem.vv, at["n1"])
+    share = [ne]
+    while len(share) < len(ENDS):
+        share = sorted(share[1:] + [share[0] // 2] * 2, reverse=True)
+    g.remote_dma_fused([transfer(T.cores[order[s]], far[sum(share[:j]):sum(share[:j + 1])], sem.cc, ends_at(T, s),
+                                 end_of(ROW[s])) for j, s in enumerate(ENDS)], local_sem=sem.ls)
+    for s in range(S):
+        to, lo, mid, hi = T.cores[order[s]], CAP * s, CAP * s + CAP // 2, CAP * (s + 1)
+        sc, sp = sem["co%d" % s], sem["pl%d" % s]
+        g.wait_ge(sem.vv, at["q%d" % s])
+        if "h%d" % s in by:
+            g.remote_dma_fused([transfer(by["h%d" % s], near, sc, codes(T.q, mid, hi), codes(T.q, mid, hi)),
+                                transfer(to, far, sc, codes(T.rc, lo, mid), codes(T.q, lo, mid))], local_sem=sem.ls)
         else:
-            tile(s)
+            sent[0] += write(g, T, topo, to, far, sc, codes(T.rc, lo, hi), codes(T.q, lo, hi))
+        if "p%d" % s in by:
+            sent[0] += write(g, T, topo, by["p%d" % s], near, sp, T.p[:, lo:hi], T.p[:, lo:hi])
+        else:
+            sent[0] += write(g, T, topo, to, far, sp, T.rp[:, lo:hi], T.p[:, lo:hi])
 
-    scanned = {}
-    for s in TURN:
+    def store(Q, s, i):
         d = rank if s == S else src[s]
-        if s == TURN[OWN_AT]:
-            work("q%d" % S)
+        Q.dma_start(T.y[:, CD * d:CD * (d + 1)], i).then_inc(sem.dy, 16)
+
+    E.wait_ge(sem.vv, at["w"])
+    vneed(at["m"])
+    picked = [0]
+    for s in TURN:
+        t = PLACE[s]
         if s == S:
             E.wait_ge(sem.vv, at["q%d" % S])
-            cq, cp, k = T.q, T.p, CAP * S
+            cq, cp = T.q, T.p
         else:
-            if not tn[0]:
-                E.wait_ge(sem.vv, at["w"])
-            E.wait_ge(sem["co%d" % d], ne)
-            E.wait_ge(sem["pl%d" % d], ne)
-            cq, cp, k = T.rc, T.rp, CAP * d
-        E.matmul_mx(T.ps[:, 512 * d:512 * d + CAP], T.wq[:, :], T.wp[:, :], cq[:, k:k + CAP], cp[:, k:k + CAP],
-                    True, True).then_inc(sem.tt, 1)
+            E.wait_ge(sem["co%d" % s], ne * (2 if "h%d" % s in by else 1))
+            E.wait_ge(sem["pl%d" % s], ne)
+            cq, cp = T.rc, T.rp
+        E.matmul_mx(T.ps[:, 512 * t:512 * t + CAP], T.wq[:, :], T.wp[:, :], cq[:, CAP * s:CAP * (s + 1)],
+                    cp[:, CAP * s:CAP * (s + 1)], True, True).then_inc(sem.tt, 1)
         tn[0] += 1
-        vneed(at["m"])
         V.wait_ge(sem.tt, tn[0])
-        b = starts(d // 2) + CAP * (d % 2) - 1
-        n = v(V.tensor_tensor_scan(T.z[:, CAP * d:CAP * (d + 1)], T.m[:, b:b + CAP],
-                                   T.ps[:, 512 * d:512 * d + CAP], -BIG, op.add, op.max))
-        scanned[d] = n
-        b = d - d % 2
-        if b in scanned and b + 1 in scanned:
-            o, i = T.ys[:, CD * b:CD * (b + 2)], T.z[:, CAP * b:CAP * (b + 2)].indirect(T.ce[:, b:b + 2])
-            if s != TURN[-1]:
-                need(A, sem.vv, av, n)
-                a_(A.activation(o, i, act.Copy))
-            else:
-                vneed(n)
-                n = v(V.tensor_copy(o, i))
-    Y.wait_ge(sem.aa, an[0])
-    Y.wait_ge(sem.vv, n)
-    Y.dma_start(T.y[:, :], T.ys[:, :]).then_inc(sem.dy, 16)
-    Y.wait_ge(sem.dy, 16)
-    g.wait_ge(sem.ls, ln_[0])
+        b = 16 + CAP * t - 1
+        n = v(V.tensor_tensor_scan(T.z[:, CAP * t:CAP * (t + 1)], T.m[:, b:b + CAP],
+                                   T.ps[:, 512 * t:512 * t + CAP], -BIG, op.add, op.max))
+        if s == TURN[-1]:
+            vneed(n)
+            Y.wait_ge(sem.vv, v(V.tensor_copy(T.yo[:, :], T.z[:, :].indirect(T.ce[:, N - 2:N]))))
+            store(Y, s, T.yo[:, CD:2 * CD])
+        elif s in PICKS:
+            lo, new, hi = PICKS[s]
+            b = picked[0] - CD * lo
+            picked[0] += CD * (hi - lo)
+            need(A, sem.vv, av, n)
+            n = a_(A.activation(T.ys[:, b + CD * lo:b + CD * hi], T.z[:, 0:CAP * hi].indirect(T.ce[:, lo:hi]),
+                                act.Copy))
+            for Q, u in zip((Y, A), range(new, hi)):
+                Q.wait_ge(sem.aa, n)
+                store(Q, PLACE.index(u), T.ys[:, b + CD * u:b + CD * (u + 1)])
+    Y.wait_ge(sem.dy, 16 * N)
+    g.wait_ge(sem.ls, sent[0])

from concourse.bass import DstId, RemoteDMATransfer
from concourse.mybir import dt, AluOpType, ActivationFunctionType

N, CD, ND, TOK, CAP = 6, 16, 64, 768, 160
S = N - 1
R = 4
ROW = [0, 1, 1, 2, 2, 3]
HALF = [None, 0, 1, 0, 1, None]
PICKS = {S: (0, 0, 2), 3: (2, 2, 3), 2: (2, 3, 5)}
PLACE = [1, 4, 3, 2, 5, 0]
LO, HI = slice(0, 64), slice(64, 128)
VW = CAP + 8
XW = 4 * (TOK + CAP)
OW = 4 * CAP // 16
MW = 2 * CAP + 16
LW = 2 * N
XA = 4 * TOK - 512
RAMP = 1024
BIG = 1.0e29
CUT = [34, 36, 16, 24, 28, 28]
VIA = [["e0", "h0", "p0", "h1", "p1", "p2"]]
ENDS = [1, 2, 3, 4]
TURN = [0, S, 3, 1, 2, 4]
ORDER = ("l0 e0 n0 d0 i g1 e1 s0 l1 p0 n1 d1 h0 c0 a0 s1 s2 s3 p1 v0 h1 p2 c1 a1 c2 a2 h2 v1 q0 c3 a3 v2 q1 c4 a4 q2 "
         "v3 p3 q3 h3 v4 c5 a5 q4 v5 u q5 m").split()

SCRATCH = {
    "cdi": ("sbuf", [128, N], "int32"),
    "cdu": ("sbuf", [128, N + 2], "uint16"),
    "cdl": ("sbuf", [128, LW * S], "uint16"),
    "cdx": ("sbuf", [128, 4], "uint16"),
    "raw": ("sbuf", [128, 2 * ND], "int32"),
    "bc": ("sbuf", [128, ND], "int32"),
    "one": ("sbuf", [128, ND], "float32"),
    "tab": ("sbuf", [128, 2 * ND], "float32"),
    "tabl": ("sbuf", [128, ND], "float32"),
    "ip": ("sbuf", [128, 4], "int32"),
    "ii": ("sbuf", [128, 8], "int32"),
    "turn": ("sbuf", [128, 4], "uint16"),
    "pf": ("sbuf", [128, 4], "float32"),
    "it16": ("sbuf", [128, 2 * CD], "float32"),
    "hb": ("sbuf", [128, 4], "float32"),
    "tri": ("sbuf", [128, 2 * CD], "float32"),
    "rst": ("sbuf", [128, 2 * CD], "float32"),
    "hold": ("sbuf", [128, CAP], "bfloat16"),
    "inc": ("sbuf", [128, CAP], "float32"),
    "neg": ("sbuf", [128, N * CD], "bfloat16"),
    "base": ("sbuf", [128, N], "float32"),
    "lm": ("sbuf", [128, R * CD], "float32"),
    "cs": ("sbuf", [128, R * CD + 8], "uint16"),
    "sg": ("sbuf", [128, R * CD], "float32"),
    "eg": ("sbuf", [128, R * CD + 8], "float32"),
    "dg": ("sbuf", [128, R * CD + 8], "float32"),
    "v": ("sbuf", [128, R * VW], "float32"),
    "f": ("sbuf", [128, R * CAP], "uint16"),
    "a": ("sbuf", [128, R * CAP], "uint16"),
    "off": ("sbuf", [128, N * OW], "uint16"),
    "xs": ("sbuf", [128, XW], "bfloat16"),
    "h": ("sbuf", [128, N * 4 * CAP], "bfloat16"),
    "qwb": ("sbuf", [128, 512], "bfloat16"),
    "wq": ("sbuf", [128, 128], "float8_e4m3fn_x4"),
    "wp": ("sbuf", [128, 128], "uint8"),
    "q": ("sbuf", [128, N * CAP], "float8_e4m3fn_x4"),
    "p": ("sbuf", [128, N * CAP], "uint8"),
    "rc": ("sbuf", [128, N * CAP], "float8_e4m3fn_x4"),
    "rp": ("sbuf", [128, N * CAP], "uint8"),
    "hl": ("sbuf", [128, 2], "uint16"),
    "cl": ("sbuf", [128, 8 * N], "uint16"),
    "ce": ("sbuf", [128, N], "uint16"),
    "m": ("sbuf", [128, 16 + MW * (N // 2)], "bfloat16"),
    "z": ("sbuf", [128, N * CAP], "float32"),
    "ys": ("sbuf", [128, N * CD], "float32"),
    "yo": ("sbuf", [128, 2 * CD], "float32"),
    "ps": ("psum", [128, 512 * N], "float32"),
}
SEMAPHORES = ["dc", "dn", "dr", "dx", "dq", "dl", "dy", "gi", "vv", "aa", "tt", "ls", "ll", "cc", "he", "go"] \
    + [k + str(i) for k in ("rq", "co", "pl") for i in range(N)]


def order_of(r, T, topo):
    chip = [topo.chip(c) for c in T.cores]
    mate = [[j for j in range(N) if topo.mates(chip[i], chip[j])][0] for i in range(N)]
    plane = sorted([j for j in range(N) if topo.same_plane(chip[r], chip[j])], key=lambda j: (j - r) % N)
    far = [mate[j] for j in plane]
    o = []
    for k in range(len(plane)):
        o += [far[k], plane[len(plane) - 1 - k]]
    return o + [mate[r]]


def helpers_of(r, T, topo):
    c, order, found = T.cores[r], order_of(r, T, topo), []
    for words in VIA:
        found.append([h for h in topo.cores_of(c) if h not in found and topo.die(h) != topo.die(c)
                      and all(topo.may_write(h, T.cores[order[int(w[1])]]) for w in words)][0])
    return found


def bits(es):
    return sum(1 << e for e in es)


def dst_id(c, topo):
    a = topo.addr(c)
    return DstId(rid=a[0], pnc=a[1])


def write(g, T, topo, to, es, sm, o, i):
    a = topo.addr(to)
    g.remote_dma(o, i, remote_sem=sm, local_sem=T.sem.ls, pid=a[1], routing_id=a[0], dma_engine_mask=bits(es))
    return len(es)


def spare(core, to, far, topo):
    return [e for e in topo.engines(core, to) if e not in topo.engines(core, far)]


def codes(buf, lo, hi):
    return buf[:, lo:hi].bitcast(dt.uint8)


def ends_at(T, s):
    return T.cl[:, 8 * PLACE[s]:8 * PLACE[s] + 1]


def helper_program(g, core, r, k, T, topo):
    order = order_of(r, T, topo)
    n = 0
    for word in VIA[k]:
        s = int(word[1])
        to = T.cores[order[s]]
        es = topo.engines(core, to)
        ne = len(spare(T.cores[r], core, to, topo))
        lo, hi = CAP * s, CAP * (s + 1)
        if word[0] == "e":
            g.wait_ge(T.sem.he, ne // len(VIA))
            n += write(g, T, topo, to, es, T.sem.cc, ends_at(T, s), T.hl[:, 0:1])
        elif word[0] == "h":
            g.wait_ge(T.sem["co%d" % s], ne)
            n += write(g, T, topo, to, es, T.sem["co%d" % s], codes(T.rc, lo + CAP // 2, hi),
                       codes(T.q, lo + CAP // 2, hi))
        else:
            g.wait_ge(T.sem["pl%d" % s], ne)
            n += write(g, T, topo, to, es, T.sem["pl%d" % s], T.rp[:, lo:hi], T.p[:, lo:hi])
    g.wait_ge(T.sem.ls, n)


def rank_program(g, core, T, topo):
    rank = T.rank_of(core)
    if rank is None:
        for r in range(N):
            hs = helpers_of(r, T, topo)
            if core in hs:
                helper_program(g, core, r, hs.index(core), T, topo)
        return
    op, act = AluOpType, ActivationFunctionType
    V, A, E, Y = g.vector, g.scalar, g.tensor, g.sync
    sem = T.sem
    orders = [order_of(r, T, topo) for r in range(N)]
    order = orders[rank]
    src = [[r for r in range(N) if r != rank and orders[r][s] == rank][0] for s in range(S)]
    helpers = helpers_of(rank, T, topo)
    by = {word: helpers[k] for k, words in enumerate(VIA) for word in words}
    far = topo.engines(core, T.cores[order[0]])
    near = spare(core, helpers[0], T.cores[order[0]], topo)
    ne = len(far)

    vn, vw, an, av, va, tn, gn, sent = [0], [0], [0], [0], [0], [0], [0], [0]

    def v(ins):
        ins.then_inc(sem.vv, 1)
        vn[0] += 1
        return vn[0]

    def a_(ins):
        ins.then_inc(sem.aa, 1)
        an[0] += 1
        return an[0]

    def gi(ins):
        ins.then_inc(sem.gi, 1)
        gn[0] += 1
        return gn[0]

    def need(Q, sm, seen, n):
        if n > seen[0]:
            Q.wait_ge(sm, n)
            seen[0] = n

    def vneed(n):
        need(V, sem.vv, vw, n)

    A.dma_start(T.raw[0:1, ND:2 * ND], T.ln[:, :]).then_inc(sem.dn, 16)
    for k in range(4):
        (Y if k % 2 == 0 else A).dma_start(T.cdi[16 * k:16 * k + 16, 0:N], T.cd[:, :]).then_inc(sem.dc, 16)
    Y.dma_start(T.raw[0:1, 0:ND], T.st[:, :]).then_inc(sem.dr, 16)
    A.dma_start(T.qwb[:, :], T.qw[:, :]).then_inc(sem.dq, 16)
    Y.dma_start(T.xs[:, 0:XA], T.x[:, 0:XA]).then_inc(sem.dx, 16)

    g_ip = gi(g.iota(T.ip[:, :], [[1, 4]], 0, 4))
    g_it = gi(g.iota(T.it16[:, :], [[0, 2], [1, CD]], 0, 0, allow_small_or_imprecise_dtypes=True))
    gi(g.iota(T.base[:, :], [[CAP, N]], -1, 0, allow_small_or_imprecise_dtypes=True))

    v_zero = v(V.memset(T.xs[:, 4 * TOK:XW], 0.0))
    V.wait_ge(sem.gi, g_ip)
    v(V.tensor_scalar(T.ii[:, 0:1], T.ip[:, 0:1], 2, 15, op.logical_shift_right, op.bitwise_and))
    v(V.tensor_scalar(T.ii[:, 1:2], T.ip[:, 0:1], 2, 3, op.logical_shift_right, op.bitwise_and))
    v(V.tensor_scalar(T.ii[:, 2:3], T.ip[:, 0:1], 4, 3, op.logical_shift_right, op.bitwise_and))
    n = v(V.tensor_scalar(T.ii[:, 4:8], T.ip[:, :], ND - 1, None, op.bitwise_and))
    v(V.memset(T.dg[:, :], 0.0))
    vneed(n)
    n = v(V.tensor_copy(T.pf[:, 0:3], T.ii[:, 0:3]))
    v(V.tensor_copy(T.turn[:, :], T.ii[:, 4:8]))
    V.wait_ge(sem.gi, g_it)
    v(V.tensor_scalar(T.rst[:, :], T.it16[:, :], 1.0, None, op.min))
    vneed(n + 1)
    v_hb = v(V.tensor_scalar(T.hb[:, :], T.it16[:, 0:4], T.pf[:, 2:3], 1.0e9, op.is_le, op.mult))

    def fill(o, n, c):
        i = T.xs[:, 4 * TOK:4 * TOK + n]
        return a_(A.activation(o, i, act.Copy) if c is None else A.activation(o, i, act.Identity, bias=c))
    need(A, sem.vv, av, v_zero)
    for k in range(2):
        fill(T.v[:, 2 * VW * k:2 * VW * (k + 1)], 2 * VW, None)
    fill(T.inc[:, 0:1], 1, None)
    fill(T.inc[:, 4:CAP:4], CAP // 4 - 1, 1.0 - 3 * RAMP)
    for u in range(1, 4):
        fill(T.inc[:, u:CAP:4], CAP // 4, 1.0 + RAMP)
    need(A, sem.vv, av, v_hb)
    for u in range(4):
        fill(T.hold[:, u:CAP:4], CAP // 4, T.hb[:, u:u + 1])
    fill(T.eg[:, 0:1], 1, None)
    a_fill = fill(T.neg[:, :], N * CD, -BIG)

    g.wait_ge(sem.dn, 16)
    g_bl = gi(g.partition_broadcast(T.bc[:, :], T.raw[0:1, ND:2 * ND], 128))

    V.wait_ge(sem.dc, 64)
    o = rank % 2
    for half in (LO, HI):
        v_cdu = v(V.tensor_copy(T.cdu[half, o:o + N], T.cdi[LO, :]))
    g.wait_ge(sem.vv, v_cdu)
    g.remote_dma_fused([RemoteDMATransfer(
        dst_ids=[dst_id(T.cores[d], topo) for d in src], dma_engine_mask=bits(far), remote_sem=sem["rq%d" % rank],
        srcs=[T.cdu[:, o:o + N]], dsts=[T.cdl[:, LW * s + N - d:LW * s + 2 * N - d] for s, d in enumerate(src)])],
        local_sem=sem.ll)
    g.sem_inc(sem.go, 1)
    Y.wait_ge(sem.go, 1)
    Y.dma_start(T.xs[:, XA:4 * TOK], T.x[:, XA:4 * TOK]).then_inc(sem.dx, 16)
    Y.wait_ge(sem.ll, ne)
    Y.wait_ge(sem.vv, v_zero)
    for k in range(2):
        Y.dma_start(T.m[:, 512 * k:512 * (k + 1)], T.xs[:, 4 * TOK:4 * TOK + 512]).then_inc(sem.dl, 16)

    V.wait_ge(sem.dr, 16)
    for u in range(ND // 16):
        n = v(V.tensor_copy(T.one[0:1, 16 * u:16 * (u + 1)], T.raw[0:1, u:ND:ND // 16]))
    g.wait_ge(sem.vv, n)
    g_bs = gi(g.partition_broadcast(T.tab[:, 0:ND], T.one[0:1, :], 128))
    V.wait_ge(sem.gi, g_bl)
    v(V.tensor_copy(T.tabl[:, :], T.bc[:, :].indirect(T.turn[:, :])))
    n = v(V.tensor_scalar(T.tri[:, :], T.it16[:, :], T.pf[:, 0:1], None, op.is_le))
    v(V.tensor_scalar(T.pf[:, 3:4], T.pf[:, 2:3], -4.0 * RAMP, T.pf[:, 1:2], op.mult, op.add))
    vneed(n)
    A.wait_ge(sem.gi, g_bs)

    own = T.cdu[:, rank + o:rank + o + 1]
    lengths = {0: (0, 1, T.cdl[:, N:N + 1]), 1: (1, 3, T.cdx[:, 0:2]), 3: (3, 4, own)}
    columns = {0: (0, 1, T.cdl[:, N:N + 1]), 1: (1, 4, T.cdx[:, 0:3])}

    def end_of(r):
        return T.cs[:, CD * (r + 1):CD * (r + 1) + 1]

    def part(s, lo, hi):
        return (T.h[:, 4 * CAP * s + 16 * lo:4 * CAP * s + 16 * hi],
                T.xs[:, :].indirect(T.off[:, OW * s + lo:OW * s + hi]))

    def starts(k):
        return 16 + MW * k

    at, waited = {}, set()

    def once(Q, name, sm, n):
        if (name, sm) not in waited:
            waited.add((name, sm))
            Q.wait_ge(sem[sm], n)

    def work(word):
        k = word[0]
        s = int(word[1:] or 0)
        c = slice(CAP * s, CAP * (s + 1))
        if k == "i":
            for t in range(1, S):
                A.wait_ge(sem["rq%d" % order[t]], ne)
            for b, half in enumerate((LO, HI)):
                x = a_(A.activation(T.cdx[half, 0:2], T.cdl[half, LW * (1 + b) + N:LW * S:2 * LW], act.Copy))
            A.wait_ge(sem.aa, x)
            need(A, sem.vv, av, at["tab"])
        elif word == "e0":
            vneed(at["tab"])
            x = v(V.tensor_copy(T.eg[:, 1:CD + 1], T.tab[:, ND:2 * ND].indirect(columns[0][2])))
        elif word == "d0":
            need(V, sem.aa, va, a_fill)
            vneed(at["e0"])
            x = v(V.tensor_tensor(T.dg[:, 0:CD], T.tab[:, 0:ND].indirect(columns[0][2]), T.eg[:, 0:CD], op.subtract))
        elif k in "ge":
            lo, hi, numbers = columns[s]
            lo, hi = CD * lo, CD * hi
            if k == "g":
                x = a_(A.activation(T.sg[:, lo:hi], T.tab[:, 0:ND].indirect(numbers), act.Copy))
            else:
                x = a_(A.activation(T.eg[:, lo + 1:hi + 1], T.tab[:, ND:2 * ND].indirect(numbers), act.Copy))
        elif k in "ln":
            lo, hi, numbers = lengths[s]
            lo, hi = CD * lo, CD * hi
            if k == "l":
                need(V, sem.aa, va, at["i"] if s == 1 else 0)
                x = v(V.tensor_tensor(T.lm[:, lo:hi], T.tabl[:, :].indirect(numbers), T.tri[:, 0:hi - lo], op.mult))
            else:
                vneed(at["l%d" % s])
                x = v(V.tensor_tensor_scan(T.cs[:, lo + 1:hi + 1], T.rst[:, 0:hi - lo], T.lm[:, lo:hi], 0.0,
                                           op.mult, op.add))
        elif k == "d":
            lo, hi = CD * columns[s][0], CD * columns[s][1]
            need(V, sem.aa, va, max(at["g%d" % s], at["e%d" % s]))
            x = v(V.tensor_tensor(T.dg[:, lo + 1:hi], T.sg[:, lo + 1:hi], T.eg[:, lo + 1:hi], op.subtract))
        elif k == "s":
            need(V, sem.aa, va, a_fill)
            vneed(max(at["n%d" % min(s, 1)], at["d%d" % min(s, 1)]))
            x = v(V.tensor_copy(T.v[:, VW * s:VW * (s + 1)].indirect(end_of(s)), T.dg[:, CD * s + 1:CD * (s + 1) + 1]))
        elif k == "p":
            need(V, sem.aa, va, a_fill)
            vneed(at["s%d" % s])
            x = v(V.tensor_tensor_scan(T.f[:, c], T.inc[:, :], T.v[:, VW * s:VW * s + CAP],
                                       (T.sg if s else T.dg)[:, CD * s:CD * s + 1], op.add, op.add))
        elif k == "h":
            vneed(at["p%d" % s])
            x = v(V.tensor_tensor_scan(T.a[:, c], T.hold[:, :], T.f[:, c], 0.0, op.max, op.min))
        elif k == "c" and HALF[s] is None:
            r = ROW[s]
            need(A, sem.vv, av, at["h%d" % r])
            x = a_(A.activation(T.off[:, OW * s:OW * (s + 1)], T.a[:, CAP * r + 3:CAP * (r + 1):4], act.Identity,
                                bias=T.pf[:, 3:4], scale=4.0))
            A.wait_ge(sem.aa, x)
        elif k == "c":
            r, both = ROW[s], slice(0, 128)
            vneed(at["h%d" % r])
            moves = [(both, both)] if HALF[s] is None else [(to, (LO, HI)[HALF[s]]) for to in (LO, HI)]
            for to, of in moves:
                x = v(V.tensor_scalar(T.off[to, OW * s:OW * (s + 1)], T.a[of, CAP * r + 3:CAP * (r + 1):4], 4.0,
                                      T.pf[of, 3:4], op.mult, op.add))
        elif k == "a":
            once(A, "A", "dx", 32)
            if HALF[s] is not None:
                need(A, sem.vv, av, at["c%d" % s])
            x = a_(A.activation(*part(s, 0, CUT[s]), act.Copy))
        elif k == "v":
            once(V, "V", "dx", 32)
            if HALF[s] is None:
                need(V, sem.aa, va, at["c%d" % s])
            else:
                vneed(at["c%d" % s])
            x = v(V.tensor_copy(*part(s, CUT[s], OW)))
        elif k == "q":
            need(V, sem.aa, va, at["a%d" % s])
            vneed(at.get("v%d" % s, 0))
            x = v(V.quantize_mx(T.q[:, c], T.p[:, c], T.h[:, 4 * CAP * s:4 * CAP * (s + 1)]))
        elif k == "w":
            V.wait_ge(sem.dq, 16)
            x = v(V.quantize_mx(T.wq[:, :], T.wp[:, :], T.qwb[:, :]))
        elif k == "u":
            V.wait_ge(sem.cc, ne * (len(VIA) + 1))
            for b, of in enumerate((LO, HI)):
                for to in (LO, HI):
                    x = v(V.tensor_tensor(T.ce[to, b:N:2], T.cl[of, 8 * b:8 * N:16], T.base[of, b:N:2], op.add))
        else:
            V.wait_ge(sem.dl, 32)
            vneed(at["u"])
            x = v(V.tensor_copy(T.m[:, 16:16 + N * CAP].indirect(T.ce[:, :]), T.neg[:, :]))
        at[word] = x

    work("l3")
    v(V.tensor_copy(T.cdx[:, 2:3], own))
    work("n3")
    work("w")
    V.wait_ge(sem.gi, g_bs)
    at["tab"] = v(V.tensor_tensor(T.tab[:, ND:2 * ND], T.tab[:, 0:ND], T.tabl[:, :], op.add))
    vneed(at["n3"])
    v(V.tensor_copy(ends_at(T, S), end_of(ROW[S])))
    V.wait_ge(sem["rq%d" % order[0]], ne)
    for word in ORDER:
        work(word)

    def transfer(to, es, sm, o, i):
        sent[0] += len(es)
        return RemoteDMATransfer(dst_ids=[dst_id(to, topo)], dma_engine_mask=bits(es), remote_sem=sm, srcs=[i], dsts=[o])

    g.wait_ge(sem.vv, max(at["n%d" % min(1, int(w[0][1]))] for w in VIA))
    k = len(near) // len(VIA)
    g.remote_dma_fused([transfer(helpers[j], near[k * j:k * (j + 1)], sem.he, T.hl[:, 0:1], end_of(ROW[int(w[0][1])]))
                        for j, w in enumerate(VIA)], local_sem=sem.ls)
    g.wait_ge(sem.vv, at["n1"])
    share = [ne]
    while len(share) < len(ENDS):
        share = sorted(share[1:] + [share[0] // 2] * 2, reverse=True)
    g.remote_dma_fused([transfer(T.cores[order[s]], far[sum(share[:j]):sum(share[:j + 1])], sem.cc, ends_at(T, s),
                                 end_of(ROW[s])) for j, s in enumerate(ENDS)], local_sem=sem.ls)
    for s in range(S):
        to, lo, mid, hi = T.cores[order[s]], CAP * s, CAP * s + CAP // 2, CAP * (s + 1)
        sc, sp = sem["co%d" % s], sem["pl%d" % s]
        g.wait_ge(sem.vv, at["q%d" % s])
        if "h%d" % s in by:
            g.remote_dma_fused([transfer(by["h%d" % s], near, sc, codes(T.q, mid, hi), codes(T.q, mid, hi)),
                                transfer(to, far, sc, codes(T.rc, lo, mid), codes(T.q, lo, mid))], local_sem=sem.ls)
        else:
            sent[0] += write(g, T, topo, to, far, sc, codes(T.rc, lo, hi), codes(T.q, lo, hi))
        if "p%d" % s in by:
            sent[0] += write(g, T, topo, by["p%d" % s], near, sp, T.p[:, lo:hi], T.p[:, lo:hi])
        else:
            sent[0] += write(g, T, topo, to, far, sp, T.rp[:, lo:hi], T.p[:, lo:hi])

    def store(Q, s, i):
        d = rank if s == S else src[s]
        Q.dma_start(T.y[:, CD * d:CD * (d + 1)], i).then_inc(sem.dy, 16)

    E.wait_ge(sem.vv, at["w"])
    vneed(at["m"])
    picked = [0]
    for s in TURN:
        t = PLACE[s]
        if s == S:
            E.wait_ge(sem.vv, at["q%d" % S])
            cq, cp = T.q, T.p
        else:
            E.wait_ge(sem["co%d" % s], ne * (2 if "h%d" % s in by else 1))
            E.wait_ge(sem["pl%d" % s], ne)
            cq, cp = T.rc, T.rp
        E.matmul_mx(T.ps[:, 512 * t:512 * t + CAP], T.wq[:, :], T.wp[:, :], cq[:, CAP * s:CAP * (s + 1)],
                    cp[:, CAP * s:CAP * (s + 1)], True, True).then_inc(sem.tt, 1)
        tn[0] += 1
        V.wait_ge(sem.tt, tn[0])
        b = 16 + CAP * t - 1
        n = v(V.tensor_tensor_scan(T.z[:, CAP * t:CAP * (t + 1)], T.m[:, b:b + CAP],
                                   T.ps[:, 512 * t:512 * t + CAP], -BIG, op.add, op.max))
        if s == TURN[-1]:
            vneed(n)
            Y.wait_ge(sem.vv, v(V.tensor_copy(T.yo[:, :], T.z[:, :].indirect(T.ce[:, N - 2:N]))))
            store(Y, s, T.yo[:, CD:2 * CD])
        elif s in PICKS:
            lo, new, hi = PICKS[s]
            b = picked[0] - CD * lo
            picked[0] += CD * (hi - lo)
            need(A, sem.vv, av, n)
            n = a_(A.activation(T.ys[:, b + CD * lo:b + CD * hi], T.z[:, 0:CAP * hi].indirect(T.ce[:, lo:hi]),
                                act.Copy))
            for Q, u in zip((Y, A), range(new, hi)):
                Q.wait_ge(sem.aa, n)
                store(Q, PLACE.index(u), T.ys[:, b + CD * u:b + CD * (u + 1)])
    Y.wait_ge(sem.dy, 16 * N)
    g.wait_ge(sem.ls, sent[0])
